import numpy as np
import ml_dtypes


def mxq(x, axis, fmt="e4m3"):
    dtype, down = {"e4m3": (ml_dtypes.float8_e4m3fn, 7), "e5m2": (ml_dtypes.float8_e5m2, 14)}[fmt]
    v = np.moveaxis(np.asarray(x, np.float32).astype(ml_dtypes.bfloat16).astype(np.float64), axis, -1)
    blocks = v.reshape(v.shape[:-1] + (-1, 32))
    amax = np.abs(blocks).max(-1, keepdims=True)
    byte = np.maximum(np.where(amax > 0, np.frexp(amax)[1] - 1 + 127, 0) - down, 1)
    scale = np.exp2(byte - 127.0)
    codes = (blocks / scale).astype(np.float32).astype(dtype).astype(np.float64)
    return np.moveaxis((codes * scale).reshape(v.shape), -1, axis)


WIDE = False


def mx_kscale(k):
    if not WIDE:
        return np.ones(k)
    levels = np.array([24, -24, 12, -12, 0])
    if k % 512:
        return np.exp2(np.random.permutation(np.resize(levels, k // 32))).repeat(32)
    a = np.empty((k // 512, 16))
    for p in range(k // 512):
        a[p, :8] = np.random.permutation(np.resize(levels, 8))
        for g in range(8):
            far = levels[np.abs(levels - a[p, g]) >= 10]
            a[p, g + 8] = far[np.random.randint(len(far))]
    return np.exp2(a.ravel()).repeat(32)


def f64(x):
    return np.asarray(x).astype(np.float64)


def striped8(idx):
    return np.concatenate([v.reshape(-1, 16).T for v in idx]).astype(np.uint16)


def unstriped8(offs):
    return np.stack([offs[16 * g:16 * g + 16].T.reshape(-1) for g in range(8)]).astype(np.int64)


E2M1 = np.array([0.0, 0.5, 1.0, 1.5, 2.0, 3.0, 4.0, 6.0, -0.0, -0.5, -1.0, -1.5, -2.0, -3.0, -4.0, -6.0])


def pack_weight(w, fmt):
    k, n = w.shape
    w = f64(np.asarray(w, np.float32).astype(ml_dtypes.bfloat16)).reshape(k // 32, 32, n)
    amax = np.abs(w).max(1)
    if fmt == "e4m3":
        byte = np.frexp(amax)[1] - 1 + 127 - 7
    else:
        mant, ex = np.frexp(amax / 6.0)
        byte = np.where(mant > 0.5, ex, ex - 1) + 127
    byte = np.clip(np.where(amax > 0, byte, 1), 1, 254)
    scaled = (w * np.exp2(127.0 - byte)[:, None, :]).reshape(k, n).astype(np.float32)
    by_word = np.ascontiguousarray(scaled.reshape(k // 512, 128, 4, n).transpose(0, 1, 3, 2))
    if fmt == "e4m3":
        words = by_word.astype(ml_dtypes.float8_e4m3fn).view(np.uint8)
    else:
        c = by_word.astype(ml_dtypes.float4_e2m1fn).view(np.uint8) & 0xF
        words = (c[..., 0::2] | (c[..., 1::2] << 4)).reshape(k // 512, 128, 2 * n)
    return np.ascontiguousarray(words), np.ascontiguousarray(byte.astype(np.uint8).reshape(k // 512, 16, n))


def unpack_weight(words, scales, fmt):
    g, _, n = scales.shape
    words = np.ascontiguousarray(words).reshape(g, 128, n, -1)
    if fmt == "e4m3":
        vals = words.view(ml_dtypes.float8_e4m3fn).astype(np.float64)
    else:
        nib = np.empty((g, 128, n, 4), np.uint8)
        nib[..., 0::2] = words & 0xF
        nib[..., 1::2] = words >> 4
        vals = E2M1[nib]
    vals = vals * np.repeat(np.exp2(scales.astype(np.float64) - 127.0), 8, axis=1)[..., None]
    return vals.transpose(0, 1, 3, 2).reshape(g * 512, n)


def planes(y):
    n, m = y.shape
    v = y.astype(np.float32).astype(ml_dtypes.bfloat16).astype(np.float64).reshape(n // 32, 32, m)
    top = np.abs(v).max(1)
    byte = np.clip(np.where(top > 0, np.frexp(top)[1] - 1 + 127 - 7, 1), 1, 254)
    codes = (v * np.exp2(127.0 - byte)[:, None, :]).reshape(n, m).astype(np.float32).astype(ml_dtypes.float8_e4m3fn).view(np.uint8)
    words = codes.reshape(n // 512, 128, 4, m).transpose(0, 1, 3, 2)
    return np.ascontiguousarray(words), np.ascontiguousarray(byte.astype(np.uint8).reshape(n // 512, 16, m))


K, R, N, T, J = 512, 1024, 512, 2048, 1024


def setup_inputs():
    n = np.random.standard_normal
    s = mx_kscale(K)[:, None]
    u = mx_kscale(R)[:, None]
    p_wg = pack_weight(n((K, R)) / np.sqrt(K) / s, "e4m3")
    p_wd = pack_weight(n((R, N)) / np.sqrt(R) / u, "e2m1")
    return {
        "xT": (n((K, T)) * s).astype(np.float32),
        "wgt": np.repeat(np.random.uniform(0.5, 2.0, (8, J)), 16, axis=0).astype(np.float32),
        "wg_words": p_wg[0],
        "wg_scales": p_wg[1],
        "wu": (n((K, R)) / np.sqrt(K) / s * u.T).astype(np.float32),
        "wd_words": p_wd[0],
        "wd_scales": p_wd[1],
        "res": (n((N, J))).astype(np.float32),
        "offs": striped8(np.stack([np.random.permutation(T)[:J] for _ in range(8)])),
    }


def reference(xT, wgt, wg_words, wg_scales, wu, wd_words, wd_scales, res, offs):
    idx = unstriped8(offs)
    rows = np.arange(K)
    xg = f64(wgt)[rows // 4 % 128] * f64(xT)[rows[:, None], idx[rows % 512 // 64]]
    xT_ = mxq(xg, 0, "e4m3")
    wg_ = unpack_weight(wg_words, wg_scales, "e4m3")
    wu_ = mxq(f64(wu), 0, "e4m3")
    ga = wg_.T @ xT_
    ub = wu_.T @ xT_
    h = np.maximum(ga, 0.0) * ub
    h_ = mxq(h, 0, "e4m3")
    wd_ = unpack_weight(wd_words, wd_scales, "e2m1")
    y = wd_.T @ h_
    out_0 = f64(res) + y
    return (out_0,) + planes(out_0)

@@ -1,0 +1,249 @@
+from contextlib import ExitStack
+
+import concourse.mybir as mybir
+
+K, R, N, T, J = 512, 1024, 512, 2048, 1024
+FLOPS = 2 * K * R * J * 2 + 2 * R * N * J
+
+F32 = mybir.dt.float32
+BF16 = mybir.dt.bfloat16
+I32 = mybir.dt.int32
+U32 = mybir.dt.uint32
+U16 = mybir.dt.uint16
+U8 = mybir.dt.uint8
+FP8X4 = mybir.dt.float8_e4m3fn_x4
+FP4X4 = mybir.dt.float4_e2m1fn_x4
+MULT = mybir.AluOpType.mult
+ADD = mybir.AluOpType.add
+RELU = mybir.ActivationFunctionType.Relu
+COPY = mybir.ActivationFunctionType.Copy
+
+P = 128
+PACK = 4
+PASS = P * PACK
+HALVES = R // PASS
+CHUNK = 128
+CHUNKS = J // CHUNK
+SLICE = 256
+SLICES = J // SLICE
+WG_ROW = 4
+OUT_WIDTHS = (256, 256, 256, 128, 128)
+LEAD = 4
+
+
+def tile_list_relu_resP_kernel(tc, xT, wgt, wg_words, wg_scales, wu, wd_words, wd_scales, res, offs, out_0, out_1, out_2):
+    nc = tc.nc
+    with ExitStack() as ctx:
+        keep = ctx.enter_context(tc.tile_pool(name="keep", bufs=1))
+        ring = ctx.enter_context(tc.tile_pool(name="ring", bufs=3))
+        psum = ctx.enter_context(tc.psum_pool(name="psum", bufs=1))
+
+        offsets = keep.tile([P, J // 16], U16, name="offsets")
+        nc.sync.dma_start(offsets[:], offs)
+
+        wgt_first = keep.tile([P, SLICE], F32, name="wgt_first")
+        wgt_rest = keep.tile([P, J - SLICE], F32, name="wgt_rest")
+        x_planes = [keep.tile([P, T], F32, name=f"x_plane{i}") for i in range(PACK)]
+        x_rows = xT.rearrange("(p i) t -> i p t", i=PACK)
+        wu_raw = [keep.tile([P, PACK, PASS], F32, name=f"wu_raw{a}") for a in range(HALVES)]
+        wu_rows = wu.rearrange("(p i) r -> p i r", i=PACK)
+        wg_raw = [keep.tile([P, PASS], I32, name=f"wg_raw{a}") for a in range(HALVES)]
+        wg_rows = wg_words[0].rearrange("p r i -> p (r i)").bitcast(I32)
+        wd_raw = keep.tile([P, HALVES, N * 2], U8, name="wd_raw")
+        scales_raw = keep.tile([P, HALVES * PASS], U8, name="scales_raw")
+        res_tiles = [keep.tile([P, PACK, J // 2], F32, name=f"res{h}") for h in range(2)]
+        res_rows = res.rearrange("(p t) j -> p t j", t=PACK)
+        out_rows = out_0.rearrange("(p t) j -> p t j", t=PACK)
+        out_words = out_1[0].rearrange("p j i -> p (j i)").bitcast(I32)
+
+        nc.gpsimd.memset(scales_raw[:].bitcast(I32), 0)
+        for q in range(4):
+            nc.gpsimd.dma_start(
+                scales_raw[32 * q : 32 * q + 4, :].bitcast(I32).rearrange("p (a n) -> p a n", a=HALVES),
+                wd_scales[:, 4 * q : 4 * q + 4, :].bitcast(I32).rearrange("a r n -> r a n"),
+            )
+
+        nc.sync.dma_start(wgt_first[:], wgt[:, 0:SLICE])
+        nc.sync.dma_start(x_planes[0][:], x_rows[0])
+        nc.sync.dma_start(wgt_rest[:], wgt[:, SLICE:J])
+        nc.sync.dma_start(x_planes[1][:], x_rows[1])
+        nc.sync.dma_start(wu_raw[0][:], wu_rows[:, :, 0:PASS])
+        nc.sync.dma_start(x_planes[2][:], x_rows[2])
+        nc.sync.dma_start(wg_raw[0][:], wg_rows[:, 0:PASS])
+        for q in range(4):
+            nc.sync.dma_start(
+                scales_raw[32 * q + WG_ROW : 32 * q + WG_ROW + 4, :].bitcast(I32),
+                wg_scales[0, 4 * q : 4 * q + 4, :].bitcast(I32),
+            )
+        nc.sync.dma_start(x_planes[3][:], x_rows[3])
+        nc.sync.dma_start(wu_raw[1][:], wu_rows[:, :, PASS:R])
+        nc.sync.dma_start(wg_raw[1][:], wg_rows[:, PASS:R])
+        nc.sync.dma_start(wd_raw[:].bitcast(I32), wd_words.bitcast(I32).rearrange("a p w -> p a w"))
+        for h in range(2):
+            nc.sync.dma_start(res_tiles[h][:], res_rows[:, :, h * (J // 2) : (h + 1) * (J // 2)])
+
+        picked = [keep.tile([P, PACK, SLICE], F32, name=f"picked{s}") for s in range(SLICES)]
+        x_codes = keep.tile([P, J], U32, name="x_codes", align_bytes=64)
+        x_scales = keep.tile([P, J], U8, name="x_scales", align_bytes=64)
+        wu_codes = [keep.tile([P, PASS], U32, name=f"wu_codes{a}", align_bytes=64) for a in range(HALVES)]
+        wu_scales = [keep.tile([P, PASS], U8, name=f"wu_scales{a}", align_bytes=64) for a in range(HALVES)]
+        wg_codes = [keep.tile([P, PASS], I32, name=f"wg_codes{a}", align_bytes=64) for a in range(HALVES)]
+        wd_codes = [keep.tile([P, N * 2], U8, name=f"wd_codes{a}", align_bytes=64) for a in range(HALVES)]
+        w_scales = keep.tile([P, HALVES * PASS], U8, name="w_scales", align_bytes=64)
+        h_codes = [keep.tile([P, J], U32, name=f"h_codes{a}", align_bytes=64) for a in range(HALVES)]
+        h_scales = [keep.tile([P, J], U8, name=f"h_scales{a}", align_bytes=64) for a in range(HALVES)]
+        out_codes = keep.tile([P, J], U32, name="out_codes", align_bytes=64)
+        out_scales = keep.tile([P, J], U8, name="out_scales", align_bytes=64)
+
+        def gather(i, s):
+            weights = wgt_first[:] if s == 0 else wgt_rest[:, (s - 1) * SLICE : s * SLICE]
+            entries = offsets[:, s * (SLICE // 16) : (s + 1) * (SLICE // 16)]
+            nc.vector.tensor_tensor(picked[s][:, i, :], x_planes[i][:].indirect(entries), weights, MULT)
+
+        def interleave(rounded, planes):
+            nc.scalar.copy(
+                rounded.rearrange("p (c e t) -> p c t e", e=4, t=PACK),
+                planes.rearrange("p t (c e) -> p c t e", e=4),
+            )
+
+        def quantise_x(s):
+            rounded = ring.tile([P, SLICE * PACK], BF16, name="x_rounded", align_bytes=64, bufs=2)
+            interleave(rounded[:], picked[s][:])
+            cols = slice(s * SLICE, (s + 1) * SLICE)
+            nc.vector.quantize_mx(x_codes[:, cols].bitcast(FP8X4), x_scales[:, cols], rounded[:])
+
+        def quantise_wu(a):
+            rounded = ring.tile([P, PASS * PACK], BF16, name="wu_rounded", align_bytes=64, bufs=2)
+            nc.scalar.activation(
+                rounded[:].rearrange("p (t m i) -> p m t i", t=PACK, i=PACK),
+                wu_raw[a][:].rearrange("p i (m t) -> p m t i", t=PACK),
+                COPY,
+            )
+            nc.vector.quantize_mx(wu_codes[a][:].bitcast(FP8X4), wu_scales[a][:], rounded[:])
+
+        def deal_wg(a):
+            nc.vector.tensor_copy(
+                wg_codes[a][:].rearrange("p (t c e) -> p c t e", t=PACK, e=4),
+                wg_raw[a][:].rearrange("p (c e t) -> p c t e", t=PACK, e=4),
+            )
+
+        def deal_scales():
+            nc.vector.tensor_copy(
+                w_scales[:].rearrange("p (a t m) -> p a t m", a=HALVES, t=PACK),
+                scales_raw[:].rearrange("p (a m t) -> p a t m", a=HALVES, t=PACK),
+            )
+
+        def deal_wd(a):
+            nc.vector.tensor_copy(
+                wd_codes[a][:].rearrange("p (t m b) -> p t m b", t=PACK, b=2),
+                wd_raw[:, a, :].rearrange("p (m t b) -> p t m b", t=PACK, b=2),
+            )
+
+        def hidden(a, c):
+            cols = slice(c * CHUNK, (c + 1) * CHUNK)
+            gate = psum.tile([P, PACK, CHUNK], F32, name="gate", bufs=3)
+            up = psum.tile([P, PACK, CHUNK], F32, name="up", bufs=3)
+            for t in range(PACK):
+                nc.tensor.matmul_mx(
+                    gate[:, t, :],
+                    lhsT=wg_codes[a][:, t * P : (t + 1) * P].bitcast(FP8X4),
+                    lhsT_scale=w_scales[WG_ROW:P, a * PASS + t * P : a * PASS + (t + 1) * P],
+                    rhs=x_codes[:, cols].bitcast(FP8X4),
+                    rhs_scale=x_scales[:, cols],
+                    start=True,
+                    stop=True,
+                )
+            for t in range(PACK):
+                nc.tensor.matmul_mx(
+                    up[:, t, :],
+                    lhsT=wu_codes[a][:, t * P : (t + 1) * P].bitcast(FP8X4),
+                    lhsT_scale=wu_scales[a][:, t * P : (t + 1) * P],
+                    rhs=x_codes[:, cols].bitcast(FP8X4),
+                    rhs_scale=x_scales[:, cols],
+                    start=True,
+                    stop=True,
+                )
+            opened = ring.tile([P, CHUNK, PACK], F32, name="opened")
+            nc.scalar.activation(opened[:], gate[:].rearrange("p t j -> p j t"), RELU)
+            rounded = ring.tile([P, CHUNK, PACK], BF16, name="h_rounded", align_bytes=64)
+            nc.vector.tensor_tensor(rounded[:], up[:].rearrange("p t j -> p j t"), opened[:], MULT)
+            return rounded
+
+        def quantise_h(a, c, rounded):
+            cols = slice(c * CHUNK, (c + 1) * CHUNK)
+            nc.vector.quantize_mx(
+                h_codes[a][:, cols].bitcast(FP8X4), h_scales[a][:, cols], rounded[:].rearrange("p j t -> p (j t)")
+            )
+
+        starts = [sum(OUT_WIDTHS[:u]) for u in range(len(OUT_WIDTHS))]
+        results = [keep.tile([P, PACK, w], F32, name=f"result{u}") for u, w in enumerate(OUT_WIDTHS)]
+
+        def down(c):
+            cols = slice(c * CHUNK, (c + 1) * CHUNK)
+            y = psum.tile([P, PACK, CHUNK], F32, name="y", bufs=2)
+            for t in range(PACK):
+                for a in range(HALVES):
+                    nc.tensor.matmul_mx(
+                        y[:, t, :],
+                        lhsT=wd_codes[a][:, 2 * t * P : 2 * (t + 1) * P].bitcast(FP4X4),
+                        lhsT_scale=w_scales[:, a * PASS + t * P : a * PASS + (t + 1) * P],
+                        rhs=h_codes[a][:, cols].bitcast(FP8X4),
+                        rhs_scale=h_scales[a][:, cols],
+                        start=(a == 0),
+                        stop=(a == HALVES - 1),
+                    )
+            u = max(v for v in range(len(starts)) if starts[v] <= c * CHUNK)
+            at = c * CHUNK - starts[u]
+            h, r0 = divmod(c * CHUNK, J // 2)
+            nc.vector.tensor_tensor(results[u][:, :, at : at + CHUNK], y[:], res_tiles[h][:, :, r0 : r0 + CHUNK], ADD)
+            if at + CHUNK == OUT_WIDTHS[u]:
+                hand_out(u)
+
+        def hand_out(u):
+            cols = slice(starts[u], starts[u] + OUT_WIDTHS[u])
+            nc.sync.dma_start(out_rows[:, :, cols], results[u][:])
+            rounded = keep.tile([P, OUT_WIDTHS[u] * PACK], BF16, name=f"out_rounded{u}", align_bytes=64)
+            interleave(rounded[:], results[u][:])
+            nc.vector.quantize_mx(out_codes[:, cols].bitcast(FP8X4), out_scales[:, cols], rounded[:])
+            nc.sync.dma_start(out_words[:, cols], out_codes[:, cols].bitcast(I32))
+
+        for i in range(2):
+            for s in range(SLICES):
+                gather(i, s)
+        for s in range(SLICES):
+            gather(2, s)
+        quantise_wu(0)
+        deal_wg(0)
+        for s in range(SLICES):
+            gather(3, s)
+            if s == 0:
+                deal_scales()
+            quantise_x(s)
+
+        units = [(0, c) for c in range(LEAD)]
+        for c in range(CHUNKS):
+            units.append((1, c))
+            if c + LEAD < CHUNKS:
+                units.append((0, c + LEAD))
+        waiting = None
+        for n, (a, c) in enumerate(units):
+            if n == 1:
+                quantise_wu(1)
+                deal_wg(1)
+            if n == 2:
+                deal_wd(0)
+                deal_wd(1)
+            rounded = hidden(a, c)
+            if waiting is not None:
+                quantise_h(*waiting)
+                if waiting[0] == 1:
+                    down(waiting[1])
+            waiting = (a, c, rounded)
+        quantise_h(*waiting)
+        down(waiting[1])
+
+        queues = (nc.sync, nc.scalar, nc.sync, nc.scalar)
+        for q in range(4):
+            queues[q].dma_start(
+                out_2[0, 4 * q : 4 * q + 4, :].bitcast(I32), out_scales[32 * q : 32 * q + 4, :].bitcast(I32)
+            )

@@ -41,8 +41,7 @@ def tile_list_relu_resP_kernel(tc, xT, wgt, wg_words, wg_scales, wu, wd_words, w
         offsets = keep.tile([P, J // 16], U16, name="offsets")
         nc.sync.dma_start(offsets[:], offs)
 
-        wgt_first = keep.tile([P, SLICE], F32, name="wgt_first")
-        wgt_rest = keep.tile([P, J - SLICE], F32, name="wgt_rest")
+        weights = keep.tile([P, J], F32, name="weights")
         x_planes = [keep.tile([P, T], F32, name=f"x_plane{i}") for i in range(PACK)]
         x_rows = xT.rearrange("(p i) t -> i p t", i=PACK)
         wu_raw = [keep.tile([P, PACK, PASS], F32, name=f"wu_raw{a}") for a in range(HALVES)]
@@ -57,32 +56,32 @@ def tile_list_relu_resP_kernel(tc, xT, wgt, wg_words, wg_scales, wu, wd_words, w
         out_words = out_1[0].rearrange("p j i -> p (j i)").bitcast(I32)
 
         nc.gpsimd.memset(scales_raw[:].bitcast(I32), 0)
-        for q in range(4):
-            nc.gpsimd.dma_start(
-                scales_raw[32 * q : 32 * q + 4, :].bitcast(I32).rearrange("p (a n) -> p a n", a=HALVES),
-                wd_scales[:, 4 * q : 4 * q + 4, :].bitcast(I32).rearrange("a r n -> r a n"),
-            )
 
-        nc.sync.dma_start(wgt_first[:], wgt[:, 0:SLICE])
+        nc.sync.dma_start(weights[:, 0:SLICE], wgt[:, 0:SLICE])
         nc.sync.dma_start(x_planes[0][:], x_rows[0])
-        nc.sync.dma_start(wgt_rest[:], wgt[:, SLICE:J])
+        nc.sync.dma_start(weights[:, SLICE:J], wgt[:, SLICE:J])
         nc.sync.dma_start(x_planes[1][:], x_rows[1])
-        nc.sync.dma_start(wu_raw[0][:], wu_rows[:, :, 0:PASS])
-        nc.sync.dma_start(x_planes[2][:], x_rows[2])
-        nc.sync.dma_start(wg_raw[0][:], wg_rows[:, 0:PASS])
         for q in range(4):
             nc.sync.dma_start(
                 scales_raw[32 * q + WG_ROW : 32 * q + WG_ROW + 4, :].bitcast(I32),
                 wg_scales[0, 4 * q : 4 * q + 4, :].bitcast(I32),
             )
+        nc.sync.dma_start(x_planes[2][:], x_rows[2])
+        nc.sync.dma_start(wu_raw[0][:], wu_rows[:, :, 0:PASS])
+        for q in range(4):
+            nc.sync.dma_start(
+                scales_raw[32 * q : 32 * q + 4, :].bitcast(I32).rearrange("p (a n) -> p a n", a=HALVES),
+                wd_scales[:, 4 * q : 4 * q + 4, :].bitcast(I32).rearrange("a r n -> r a n"),
+            )
+        nc.sync.dma_start(wg_raw[0][:], wg_rows[:, 0:PASS])
         nc.sync.dma_start(x_planes[3][:], x_rows[3])
+        nc.sync.dma_start(wd_raw[:].bitcast(I32), wd_words.bitcast(I32).rearrange("a p w -> p a w"))
         nc.sync.dma_start(wu_raw[1][:], wu_rows[:, :, PASS:R])
         nc.sync.dma_start(wg_raw[1][:], wg_rows[:, PASS:R])
-        nc.sync.dma_start(wd_raw[:].bitcast(I32), wd_words.bitcast(I32).rearrange("a p w -> p a w"))
         for h in range(2):
             nc.sync.dma_start(res_tiles[h][:], res_rows[:, :, h * (J // 2) : (h + 1) * (J // 2)])
 
-        picked = [keep.tile([P, PACK, SLICE], F32, name=f"picked{s}") for s in range(SLICES)]
+        picked = [keep.tile([P, PACK, J // 2], F32, name=f"picked{s}", align_bytes=64) for s in range(2)]
         x_codes = keep.tile([P, J], U32, name="x_codes", align_bytes=64)
         x_scales = keep.tile([P, J], U8, name="x_scales", align_bytes=64)
         wu_codes = [keep.tile([P, PASS], U32, name=f"wu_codes{a}", align_bytes=64) for a in range(HALVES)]
@@ -95,22 +94,26 @@ def tile_list_relu_resP_kernel(tc, xT, wgt, wg_words, wg_scales, wu, wd_words, w
         out_codes = keep.tile([P, J], U32, name="out_codes", align_bytes=64)
         out_scales = keep.tile([P, J], U8, name="out_scales", align_bytes=64)
 
-        def gather(i, s):
-            weights = wgt_first[:] if s == 0 else wgt_rest[:, (s - 1) * SLICE : s * SLICE]
-            entries = offsets[:, s * (SLICE // 16) : (s + 1) * (SLICE // 16)]
-            nc.vector.tensor_tensor(picked[s][:, i, :], x_planes[i][:].indirect(entries), weights, MULT)
+        def gather(i, j0, width):
+            s, at = divmod(j0, J // 2)
+            entries = offsets[:, j0 // 16 : (j0 + width) // 16]
+            nc.vector.tensor_tensor(picked[s][:, i, at : at + width], x_planes[i][:].indirect(entries), weights[:, j0 : j0 + width], MULT)
 
-        def interleave(rounded, planes):
-            nc.scalar.copy(
+        def interleave(rounded, planes, copy=nc.scalar.copy):
+            copy(
                 rounded.rearrange("p (c e t) -> p c t e", e=4, t=PACK),
                 planes.rearrange("p t (c e) -> p c t e", e=4),
             )
 
-        def quantise_x(s):
-            rounded = ring.tile([P, SLICE * PACK], BF16, name="x_rounded", align_bytes=64, bufs=2)
-            interleave(rounded[:], picked[s][:])
-            cols = slice(s * SLICE, (s + 1) * SLICE)
-            nc.vector.quantize_mx(x_codes[:, cols].bitcast(FP8X4), x_scales[:, cols], rounded[:])
+        def quantise_x(j0, width):
+            s, at = divmod(j0, J // 2)
+            if j0 < SLICE:
+                rounded = picked[1][:, PACK - 1, 2 * j0 : 2 * (j0 + width)].bitcast(BF16)
+            else:
+                rounded = ring.tile([P, width * PACK], BF16, name="x_rounded", align_bytes=64)[:]
+            interleave(rounded, picked[s][:, :, at : at + width])
+            cols = slice(j0, j0 + width)
+            nc.vector.quantize_mx(x_codes[:, cols].bitcast(FP8X4), x_scales[:, cols], rounded)
 
         def quantise_wu(a):
             rounded = ring.tile([P, PASS * PACK], BF16, name="wu_rounded", align_bytes=64, bufs=2)
@@ -135,11 +138,11 @@ def tile_list_relu_resP_kernel(tc, xT, wgt, wg_words, wg_scales, wu, wd_words, w
 
         def deal_wd(a):
             nc.vector.tensor_copy(
-                wd_codes[a][:].rearrange("p (t m b) -> p t m b", t=PACK, b=2),
-                wd_raw[:, a, :].rearrange("p (m t b) -> p t m b", t=PACK, b=2),
+                wd_codes[a][:].bitcast(U16).rearrange("p (t m) -> p t m", t=PACK),
+                wd_raw[:, a, :].bitcast(U16).rearrange("p (m t) -> p t m", t=PACK),
             )
 
-        def hidden(a, c):
+        def hidden(a, c, rounded):
             cols = slice(c * CHUNK, (c + 1) * CHUNK)
             gate = psum.tile([P, PACK, CHUNK], F32, name="gate", bufs=3)
             up = psum.tile([P, PACK, CHUNK], F32, name="up", bufs=3)
@@ -165,15 +168,22 @@ def tile_list_relu_resP_kernel(tc, xT, wgt, wg_words, wg_scales, wu, wd_words, w
                 )
             opened = ring.tile([P, CHUNK, PACK], F32, name="opened")
             nc.scalar.activation(opened[:], gate[:].rearrange("p t j -> p j t"), RELU)
-            rounded = ring.tile([P, CHUNK, PACK], BF16, name="h_rounded", align_bytes=64)
-            nc.vector.tensor_tensor(rounded[:], up[:].rearrange("p t j -> p j t"), opened[:], MULT)
+            nc.vector.tensor_tensor(
+                rounded.rearrange("p (j t) -> p j t", t=PACK), up[:].rearrange("p t j -> p j t"), opened[:], MULT
+            )
+
+        def hidden_group(a, c0, count):
+            rounded = ring.tile([P, count * CHUNK * PACK], BF16, name="h_rounded", align_bytes=64)
+            for c in range(count):
+                hidden(a, c0 + c, rounded[:, c * CHUNK * PACK : (c + 1) * CHUNK * PACK])
             return rounded
 
-        def quantise_h(a, c, rounded):
-            cols = slice(c * CHUNK, (c + 1) * CHUNK)
-            nc.vector.quantize_mx(
-                h_codes[a][:, cols].bitcast(FP8X4), h_scales[a][:, cols], rounded[:].rearrange("p j t -> p (j t)")
-            )
+        def quantise_h(a, c0, count, rounded):
+            cols = slice(c0 * CHUNK, (c0 + count) * CHUNK)
+            nc.vector.quantize_mx(h_codes[a][:, cols].bitcast(FP8X4), h_scales[a][:, cols], rounded[:])
+            if a == HALVES - 1:
+                for c in range(c0, c0 + count):
+                    down(c)
 
         starts = [sum(OUT_WIDTHS[:u]) for u in range(len(OUT_WIDTHS))]
         results = [keep.tile([P, PACK, w], F32, name=f"result{u}") for u, w in enumerate(OUT_WIDTHS)]
@@ -181,16 +191,16 @@ def tile_list_relu_resP_kernel(tc, xT, wgt, wg_words, wg_scales, wu, wd_words, w
         def down(c):
             cols = slice(c * CHUNK, (c + 1) * CHUNK)
             y = psum.tile([P, PACK, CHUNK], F32, name="y", bufs=2)
-            for t in range(PACK):
-                for a in range(HALVES):
+            for a in range(HALVES):
+                for t in range(PACK):
                     nc.tensor.matmul_mx(
                         y[:, t, :],
                         lhsT=wd_codes[a][:, 2 * t * P : 2 * (t + 1) * P].bitcast(FP4X4),
                         lhsT_scale=w_scales[:, a * PASS + t * P : a * PASS + (t + 1) * P],
                         rhs=h_codes[a][:, cols].bitcast(FP8X4),
                         rhs_scale=h_scales[a][:, cols],
-                        start=(a == 0),
-                        stop=(a == HALVES - 1),
+                        start=(a == 0 and t == 0),
+                        stop=(a == HALVES - 1 and t == PACK - 1),
                     )
             u = max(v for v in range(len(starts)) if starts[v] <= c * CHUNK)
             at = c * CHUNK - starts[u]
@@ -203,44 +213,42 @@ def tile_list_relu_resP_kernel(tc, xT, wgt, wg_words, wg_scales, wu, wd_words, w
             cols = slice(starts[u], starts[u] + OUT_WIDTHS[u])
             nc.sync.dma_start(out_rows[:, :, cols], results[u][:])
             rounded = keep.tile([P, OUT_WIDTHS[u] * PACK], BF16, name=f"out_rounded{u}", align_bytes=64)
-            interleave(rounded[:], results[u][:])
+            interleave(rounded[:], results[u][:], nc.vector.tensor_copy if u == len(OUT_WIDTHS) - 1 else nc.scalar.copy)
             nc.vector.quantize_mx(out_codes[:, cols].bitcast(FP8X4), out_scales[:, cols], rounded[:])
             nc.sync.dma_start(out_words[:, cols], out_codes[:, cols].bitcast(I32))
 
-        for i in range(2):
-            for s in range(SLICES):
-                gather(i, s)
-        for s in range(SLICES):
-            gather(2, s)
-        quantise_wu(0)
+        gather(0, 0, SLICE)
+        gather(0, SLICE, SLICE)
+        gather(0, J // 2, J // 2)
+        for i in range(1, PACK - 1):
+            for s in range(2):
+                gather(i, s * (J // 2), J // 2)
+        deal_scales()
         deal_wg(0)
-        for s in range(SLICES):
-            gather(3, s)
-            if s == 0:
-                deal_scales()
-            quantise_x(s)
+        quantise_wu(0)
+        last = PACK - 1
+        for j0 in (0, CHUNK):
+            gather(last, j0, CHUNK)
+            quantise_x(j0, CHUNK)
+        for s in range(1, SLICES):
+            gather(last, s * SLICE, SLICE)
 
-        units = [(0, c) for c in range(LEAD)]
-        for c in range(CHUNKS):
-            units.append((1, c))
-            if c + LEAD < CHUNKS:
-                units.append((0, c + LEAD))
+        groups = [(0, 0, 2), (0, 2, 2), (1, 0, 2), (0, 4, 2), (1, 2, 2), (0, 6, 2), (1, 4, 2), (1, 6, 1), (1, 7, 1)]
         waiting = None
-        for n, (a, c) in enumerate(units):
+        for n, (a, c0, count) in enumerate(groups):
+            if a == 0 and c0 > 0:
+                quantise_x(c0 * CHUNK, SLICE)
             if n == 1:
-                quantise_wu(1)
-                deal_wg(1)
-            if n == 2:
                 deal_wd(0)
                 deal_wd(1)
-            rounded = hidden(a, c)
+            if (a, c0) == (1, 0):
+                quantise_wu(1)
+                deal_wg(1)
+            rounded = hidden_group(a, c0, count)
             if waiting is not None:
                 quantise_h(*waiting)
-                if waiting[0] == 1:
-                    down(waiting[1])
-            waiting = (a, c, rounded)
+            waiting = (a, c0, count, rounded)
         quantise_h(*waiting)
-        down(waiting[1])
 
         queues = (nc.sync, nc.scalar, nc.sync, nc.scalar)
         for q in range(4):

@@ -27,6 +27,7 @@ CHUNKS = J // CHUNK
 SLICE = 256
 SLICES = J // SLICE
 WG_ROW = 4
+WU_PIECE = PASS // 2
 OUT_WIDTHS = (256, 256, 256, 128, 128)
 LEAD = 4
 
@@ -44,11 +45,11 @@ def tile_list_relu_resP_kernel(tc, xT, wgt, wg_words, wg_scales, wu, wd_words, w
         weights = keep.tile([P, J], F32, name="weights")
         x_planes = [keep.tile([P, T], F32, name=f"x_plane{i}") for i in range(PACK)]
         x_rows = xT.rearrange("(p i) t -> i p t", i=PACK)
-        wu_raw = [keep.tile([P, PACK, PASS], F32, name=f"wu_raw{a}") for a in range(HALVES)]
+        wu_raw = [keep.tile([P, PACK, WU_PIECE], F32, name=f"wu_raw{u}") for u in range(R // WU_PIECE)]
         wu_rows = wu.rearrange("(p i) r -> p i r", i=PACK)
         wg_raw = [keep.tile([P, PASS], I32, name=f"wg_raw{a}") for a in range(HALVES)]
         wg_rows = wg_words[0].rearrange("p r i -> p (r i)").bitcast(I32)
-        wd_raw = keep.tile([P, HALVES, N * 2], U8, name="wd_raw")
+        wd_raw = keep.tile([P, HALVES * N * 2], U8, name="wd_raw")
         scales_raw = keep.tile([P, HALVES * PASS], U8, name="scales_raw")
         res_tiles = [keep.tile([P, PACK, J // 2], F32, name=f"res{h}") for h in range(2)]
         res_rows = res.rearrange("(p t) j -> p t j", t=PACK)
@@ -67,16 +68,18 @@ def tile_list_relu_resP_kernel(tc, xT, wgt, wg_words, wg_scales, wu, wd_words, w
                 wg_scales[0, 4 * q : 4 * q + 4, :].bitcast(I32),
             )
         nc.sync.dma_start(x_planes[2][:], x_rows[2])
-        nc.sync.dma_start(wu_raw[0][:], wu_rows[:, :, 0:PASS])
+        nc.sync.dma_start(x_planes[3][:], x_rows[3])
         for q in range(4):
             nc.sync.dma_start(
                 scales_raw[32 * q : 32 * q + 4, :].bitcast(I32).rearrange("p (a n) -> p a n", a=HALVES),
                 wd_scales[:, 4 * q : 4 * q + 4, :].bitcast(I32).rearrange("a r n -> r a n"),
             )
+        for u in range(2):
+            nc.sync.dma_start(wu_raw[u][:], wu_rows[:, :, u * WU_PIECE : (u + 1) * WU_PIECE])
         nc.sync.dma_start(wg_raw[0][:], wg_rows[:, 0:PASS])
-        nc.sync.dma_start(x_planes[3][:], x_rows[3])
-        nc.sync.dma_start(wd_raw[:].bitcast(I32), wd_words.bitcast(I32).rearrange("a p w -> p a w"))
-        nc.sync.dma_start(wu_raw[1][:], wu_rows[:, :, PASS:R])
+        nc.sync.dma_start(wd_raw[:].bitcast(I32).rearrange("p (a w) -> p a w", a=HALVES), wd_words.bitcast(I32).rearrange("a p w -> p a w"))
+        for u in range(2, 4):
+            nc.sync.dma_start(wu_raw[u][:], wu_rows[:, :, u * WU_PIECE : (u + 1) * WU_PIECE])
         nc.sync.dma_start(wg_raw[1][:], wg_rows[:, PASS:R])
         for h in range(2):
             nc.sync.dma_start(res_tiles[h][:], res_rows[:, :, h * (J // 2) : (h + 1) * (J // 2)])
@@ -87,7 +90,7 @@ def tile_list_relu_resP_kernel(tc, xT, wgt, wg_words, wg_scales, wu, wd_words, w
         wu_codes = [keep.tile([P, PASS], U32, name=f"wu_codes{a}", align_bytes=64) for a in range(HALVES)]
         wu_scales = [keep.tile([P, PASS], U8, name=f"wu_scales{a}", align_bytes=64) for a in range(HALVES)]
         wg_codes = [keep.tile([P, PASS], I32, name=f"wg_codes{a}", align_bytes=64) for a in range(HALVES)]
-        wd_codes = [keep.tile([P, N * 2], U8, name=f"wd_codes{a}", align_bytes=64) for a in range(HALVES)]
+        wd_codes = keep.tile([P, HALVES * N * 2], U8, name="wd_codes", align_bytes=64)
         w_scales = keep.tile([P, HALVES * PASS], U8, name="w_scales", align_bytes=64)
         h_codes = [keep.tile([P, J], U32, name=f"h_codes{a}", align_bytes=64) for a in range(HALVES)]
         h_scales = [keep.tile([P, J], U8, name=f"h_scales{a}", align_bytes=64) for a in range(HALVES)]
@@ -107,21 +110,19 @@ def tile_list_relu_resP_kernel(tc, xT, wgt, wg_words, wg_scales, wu, wd_words, w
 
         def quantise_x(j0, width):
             s, at = divmod(j0, J // 2)
-            if j0 < SLICE:
-                rounded = picked[1][:, PACK - 1, 2 * j0 : 2 * (j0 + width)].bitcast(BF16)
-            else:
-                rounded = ring.tile([P, width * PACK], BF16, name="x_rounded", align_bytes=64)[:]
+            rounded = ring.tile([P, width * PACK], BF16, name="x_rounded", align_bytes=64)[:]
             interleave(rounded, picked[s][:, :, at : at + width])
             cols = slice(j0, j0 + width)
             nc.vector.quantize_mx(x_codes[:, cols].bitcast(FP8X4), x_scales[:, cols], rounded)
 
         def quantise_wu(a):
             rounded = ring.tile([P, PASS * PACK], BF16, name="wu_rounded", align_bytes=64, bufs=2)
-            nc.scalar.activation(
-                rounded[:].rearrange("p (t m i) -> p m t i", t=PACK, i=PACK),
-                wu_raw[a][:].rearrange("p i (m t) -> p m t i", t=PACK),
-                COPY,
-            )
+            for u in range(2):
+                nc.scalar.activation(
+                    rounded[:].rearrange("p (t m i) -> p m t i", t=PACK, i=PACK)[:, u * (P // 2) : (u + 1) * (P // 2)],
+                    wu_raw[2 * a + u][:].rearrange("p i (m t) -> p m t i", t=PACK),
+                    COPY,
+                )
             nc.vector.quantize_mx(wu_codes[a][:].bitcast(FP8X4), wu_scales[a][:], rounded[:])
 
         def deal_wg(a):
@@ -136,10 +137,10 @@ def tile_list_relu_resP_kernel(tc, xT, wgt, wg_words, wg_scales, wu, wd_words, w
                 scales_raw[:].rearrange("p (a m t) -> p a t m", a=HALVES, t=PACK),
             )
 
-        def deal_wd(a):
+        def deal_wd():
             nc.vector.tensor_copy(
-                wd_codes[a][:].bitcast(U16).rearrange("p (t m) -> p t m", t=PACK),
-                wd_raw[:, a, :].bitcast(U16).rearrange("p (m t) -> p t m", t=PACK),
+                wd_codes[:].bitcast(U16).rearrange("p (a t m) -> p a t m", a=HALVES, t=PACK),
+                wd_raw[:].bitcast(U16).rearrange("p (a m t) -> p a t m", a=HALVES, t=PACK),
             )
 
         def hidden(a, c, rounded):
@@ -195,7 +196,7 @@ def tile_list_relu_resP_kernel(tc, xT, wgt, wg_words, wg_scales, wu, wd_words, w
                 for t in range(PACK):
                     nc.tensor.matmul_mx(
                         y[:, t, :],
-                        lhsT=wd_codes[a][:, 2 * t * P : 2 * (t + 1) * P].bitcast(FP4X4),
+                        lhsT=wd_codes[:, 2 * (a * PASS + t * P) : 2 * (a * PASS + (t + 1) * P)].bitcast(FP4X4),
                         lhsT_scale=w_scales[:, a * PASS + t * P : a * PASS + (t + 1) * P],
                         rhs=h_codes[a][:, cols].bitcast(FP8X4),
                         rhs_scale=h_scales[a][:, cols],
@@ -215,7 +216,9 @@ def tile_list_relu_resP_kernel(tc, xT, wgt, wg_words, wg_scales, wu, wd_words, w
             rounded = keep.tile([P, OUT_WIDTHS[u] * PACK], BF16, name=f"out_rounded{u}", align_bytes=64)
             interleave(rounded[:], results[u][:], nc.vector.tensor_copy if u == len(OUT_WIDTHS) - 1 else nc.scalar.copy)
             nc.vector.quantize_mx(out_codes[:, cols].bitcast(FP8X4), out_scales[:, cols], rounded[:])
-            nc.sync.dma_start(out_words[:, cols], out_codes[:, cols].bitcast(I32))
+            end = cols.stop
+            if end % SLICE == 0:
+                nc.sync.dma_start(out_words[:, end - SLICE : end], out_codes[:, end - SLICE : end].bitcast(I32))
 
         gather(0, 0, SLICE)
         gather(0, SLICE, SLICE)
@@ -223,15 +226,12 @@ def tile_list_relu_resP_kernel(tc, xT, wgt, wg_words, wg_scales, wu, wd_words, w
         for i in range(1, PACK - 1):
             for s in range(2):
                 gather(i, s * (J // 2), J // 2)
+        for s in range(SLICES):
+            gather(PACK - 1, s * SLICE, SLICE)
+        quantise_wu(0)
+        quantise_x(0, SLICE)
         deal_scales()
         deal_wg(0)
-        quantise_wu(0)
-        last = PACK - 1
-        for j0 in (0, CHUNK):
-            gather(last, j0, CHUNK)
-            quantise_x(j0, CHUNK)
-        for s in range(1, SLICES):
-            gather(last, s * SLICE, SLICE)
 
         groups = [(0, 0, 2), (0, 2, 2), (1, 0, 2), (0, 4, 2), (1, 2, 2), (0, 6, 2), (1, 4, 2), (1, 6, 1), (1, 7, 1)]
         waiting = None
@@ -239,8 +239,7 @@ def tile_list_relu_resP_kernel(tc, xT, wgt, wg_words, wg_scales, wu, wd_words, w
             if a == 0 and c0 > 0:
                 quantise_x(c0 * CHUNK, SLICE)
             if n == 1:
-                deal_wd(0)
-                deal_wd(1)
+                deal_wd()
             if (a, c0) == (1, 0):
                 quantise_wu(1)
                 deal_wg(1)

@@ -119,8 +119,8 @@ def tile_list_relu_resP_kernel(tc, xT, wgt, wg_words, wg_scales, wu, wd_words, w
             rounded = ring.tile([P, PASS * PACK], BF16, name="wu_rounded", align_bytes=64, bufs=2)
             for u in range(2):
                 nc.scalar.activation(
-                    rounded[:].rearrange("p (t m i) -> p m t i", t=PACK, i=PACK)[:, u * (P // 2) : (u + 1) * (P // 2)],
-                    wu_raw[2 * a + u][:].rearrange("p i (m t) -> p m t i", t=PACK),
+                    rounded[:].rearrange("p (t m i) -> p m i t", t=PACK, i=PACK)[:, u * (P // 2) : (u + 1) * (P // 2)],
+                    wu_raw[2 * a + u][:].rearrange("p i (m t) -> p m i t", t=PACK),
                     COPY,
                 )
             nc.vector.quantize_mx(wu_codes[a][:].bitcast(FP8X4), wu_scales[a][:], rounded[:])
@@ -167,10 +167,13 @@ def tile_list_relu_resP_kernel(tc, xT, wgt, wg_words, wg_scales, wu, wd_words, w
                     start=True,
                     stop=True,
                 )
-            opened = ring.tile([P, CHUNK, PACK], F32, name="opened")
-            nc.scalar.activation(opened[:], gate[:].rearrange("p t j -> p j t"), RELU)
+            opened = ring.tile([P, CHUNK // 2, PACK, 2], F32, name="opened")
+            nc.scalar.activation(opened[:], gate[:].rearrange("p t (c e) -> p c t e", e=2), RELU)
             nc.vector.tensor_tensor(
-                rounded.rearrange("p (j t) -> p j t", t=PACK), up[:].rearrange("p t j -> p j t"), opened[:], MULT
+                rounded.rearrange("p (c e t) -> p c t e", e=2, t=PACK),
+                up[:].rearrange("p t (c e) -> p c t e", e=2),
+                opened[:],
+                MULT,
             )
 
         def hidden_group(a, c0, count):

@@ -26,10 +26,12 @@ CHUNK = 128
 CHUNKS = J // CHUNK
 SLICE = 256
 SLICES = J // SLICE
-WG_ROW = 4
+WG_ROW = 8
 WU_PIECE = PASS // 2
 OUT_WIDTHS = (256, 256, 256, 128, 128)
-LEAD = 4
+PICK_WIDTHS = (1024,)
+GPSIMD_CHUNKS = ()
+X_ROUNDED_IN = {0: "x_first", 128: "wu_raw1", 256: "wu_rounded0", 512: "wu_raw3", 768: "wu_raw3"}
 
 
 def tile_list_relu_resP_kernel(tc, xT, wgt, wg_words, wg_scales, wu, wd_words, wd_scales, res, offs, out_0, out_1, out_2):
@@ -40,65 +42,78 @@ def tile_list_relu_resP_kernel(tc, xT, wgt, wg_words, wg_scales, wu, wd_words, w
         psum = ctx.enter_context(tc.psum_pool(name="psum", bufs=1))
 
         offsets = keep.tile([P, J // 16], U16, name="offsets")
-        nc.sync.dma_start(offsets[:], offs)
 
         weights = keep.tile([P, J], F32, name="weights")
         x_planes = [keep.tile([P, T], F32, name=f"x_plane{i}") for i in range(PACK)]
         x_rows = xT.rearrange("(p i) t -> i p t", i=PACK)
-        wu_raw = [keep.tile([P, PACK, WU_PIECE], F32, name=f"wu_raw{u}") for u in range(R // WU_PIECE)]
+        wu_raw = [keep.tile([P, PACK, WU_PIECE], F32, name=f"wu_raw{u}", tag=f"wu_raw{u}", align_bytes=64) for u in range(R // WU_PIECE)]
         wu_rows = wu.rearrange("(p i) r -> p i r", i=PACK)
         wg_raw = [keep.tile([P, PASS], I32, name=f"wg_raw{a}") for a in range(HALVES)]
         wg_rows = wg_words[0].rearrange("p r i -> p (r i)").bitcast(I32)
         wd_raw = keep.tile([P, HALVES * N * 2], U8, name="wd_raw")
-        scales_raw = keep.tile([P, HALVES * PASS], U8, name="scales_raw")
+        scales_raw = keep.tile([P, PASS], U8, name="scales_raw")
+        wd_late_scales = keep.tile([P, PASS], U8, name="wd_late_scales", align_bytes=64)
         res_tiles = [keep.tile([P, PACK, J // 2], F32, name=f"res{h}") for h in range(2)]
         res_rows = res.rearrange("(p t) j -> p t j", t=PACK)
         out_rows = out_0.rearrange("(p t) j -> p t j", t=PACK)
         out_words = out_1[0].rearrange("p j i -> p (j i)").bitcast(I32)
 
         nc.gpsimd.memset(scales_raw[:].bitcast(I32), 0)
+        nc.gpsimd.memset(wd_late_scales[:].bitcast(I32), 0)
 
-        nc.sync.dma_start(weights[:, 0:SLICE], wgt[:, 0:SLICE])
         nc.sync.dma_start(x_planes[0][:], x_rows[0])
+        nc.sync.dma_start(offsets[:], offs)
+        nc.sync.dma_start(weights[:, 0:SLICE], wgt[:, 0:SLICE])
         nc.sync.dma_start(weights[:, SLICE:J], wgt[:, SLICE:J])
         nc.sync.dma_start(x_planes[1][:], x_rows[1])
         for q in range(4):
             nc.sync.dma_start(
-                scales_raw[32 * q + WG_ROW : 32 * q + WG_ROW + 4, :].bitcast(I32),
-                wg_scales[0, 4 * q : 4 * q + 4, :].bitcast(I32),
+                scales_raw[32 * q + WG_ROW : 32 * q + WG_ROW + 8, :].bitcast(I32),
+                wg_scales[0, 4 * q : 4 * q + 4, :].bitcast(I32).rearrange("r (a n) -> a r n", a=HALVES),
             )
         nc.sync.dma_start(x_planes[2][:], x_rows[2])
         nc.sync.dma_start(x_planes[3][:], x_rows[3])
         for q in range(4):
             nc.sync.dma_start(
-                scales_raw[32 * q : 32 * q + 4, :].bitcast(I32).rearrange("p (a n) -> p a n", a=HALVES),
-                wd_scales[:, 4 * q : 4 * q + 4, :].bitcast(I32).rearrange("a r n -> r a n"),
+                scales_raw[32 * q : 32 * q + 8, :].bitcast(I32),
+                wd_scales[:, 4 * q : 4 * q + 4, :].bitcast(I32),
             )
         for u in range(2):
             nc.sync.dma_start(wu_raw[u][:], wu_rows[:, :, u * WU_PIECE : (u + 1) * WU_PIECE])
         nc.sync.dma_start(wg_raw[0][:], wg_rows[:, 0:PASS])
-        nc.sync.dma_start(wd_raw[:].bitcast(I32).rearrange("p (a w) -> p a w", a=HALVES), wd_words.bitcast(I32).rearrange("a p w -> p a w"))
         for u in range(2, 4):
             nc.sync.dma_start(wu_raw[u][:], wu_rows[:, :, u * WU_PIECE : (u + 1) * WU_PIECE])
         nc.sync.dma_start(wg_raw[1][:], wg_rows[:, PASS:R])
+        nc.sync.dma_start(wd_raw[:].bitcast(I32).rearrange("p (a w) -> p a w", a=HALVES), wd_words.bitcast(I32).rearrange("a p w -> p a w"))
         for h in range(2):
             nc.sync.dma_start(res_tiles[h][:], res_rows[:, :, h * (J // 2) : (h + 1) * (J // 2)])
 
-        picked = [keep.tile([P, PACK, J // 2], F32, name=f"picked{s}", align_bytes=64) for s in range(2)]
+        picked = [keep.tile([P, PACK, w], F32, name=f"picked{s}", align_bytes=64) for s, w in enumerate(PICK_WIDTHS)]
+        pick_starts = [sum(PICK_WIDTHS[:s]) for s in range(len(PICK_WIDTHS))]
+
+        def place(j0):
+            s = max(v for v in range(len(pick_starts)) if pick_starts[v] <= j0)
+            return s, j0 - pick_starts[s]
+
         x_codes = keep.tile([P, J], U32, name="x_codes", align_bytes=64)
         x_scales = keep.tile([P, J], U8, name="x_scales", align_bytes=64)
         wu_codes = [keep.tile([P, PASS], U32, name=f"wu_codes{a}", align_bytes=64) for a in range(HALVES)]
         wu_scales = [keep.tile([P, PASS], U8, name=f"wu_scales{a}", align_bytes=64) for a in range(HALVES)]
         wg_codes = [keep.tile([P, PASS], I32, name=f"wg_codes{a}", align_bytes=64) for a in range(HALVES)]
         wd_codes = keep.tile([P, HALVES * N * 2], U8, name="wd_codes", align_bytes=64)
-        w_scales = keep.tile([P, HALVES * PASS], U8, name="w_scales", align_bytes=64)
-        h_codes = [keep.tile([P, J], U32, name=f"h_codes{a}", align_bytes=64) for a in range(HALVES)]
-        h_scales = [keep.tile([P, J], U8, name=f"h_scales{a}", align_bytes=64) for a in range(HALVES)]
+        w_scales = keep.tile([P, PASS], U8, name="w_scales", align_bytes=64)
+        h_rounded = [keep.tile([P, HALVES * SLICE * PACK], BF16, name=f"h_rounded{s}", align_bytes=64) for s in range(SLICES)]
+        h_codes = [keep.tile([P, HALVES * SLICE], U32, name=f"h_codes{s}", align_bytes=64) for s in range(SLICES)]
+        h_scales = [keep.tile([P, HALVES * SLICE], U8, name=f"h_scales{s}", align_bytes=64) for s in range(SLICES)]
+
+        def h_place(a, c):
+            s, half = divmod(c, 2)
+            return s, a * SLICE + half * CHUNK
         out_codes = keep.tile([P, J], U32, name="out_codes", align_bytes=64)
         out_scales = keep.tile([P, J], U8, name="out_scales", align_bytes=64)
 
         def gather(i, j0, width):
-            s, at = divmod(j0, J // 2)
+            s, at = place(j0)
             entries = offsets[:, j0 // 16 : (j0 + width) // 16]
             nc.vector.tensor_tensor(picked[s][:, i, at : at + width], x_planes[i][:].indirect(entries), weights[:, j0 : j0 + width], MULT)
 
@@ -109,14 +124,14 @@ def tile_list_relu_resP_kernel(tc, xT, wgt, wg_words, wg_scales, wu, wd_words, w
             )
 
         def quantise_x(j0, width):
-            s, at = divmod(j0, J // 2)
-            rounded = ring.tile([P, width * PACK], BF16, name="x_rounded", align_bytes=64)[:]
-            interleave(rounded, picked[s][:, :, at : at + width])
+            s, at = place(j0)
+            rounded = keep.tile([P, width * PACK], BF16, name="x_rounded", tag=X_ROUNDED_IN[j0], align_bytes=64)[:]
+            interleave(rounded, picked[s][:, :, at : at + width], nc.vector.tensor_copy if j0 == SLICE else nc.scalar.copy)
             cols = slice(j0, j0 + width)
             nc.vector.quantize_mx(x_codes[:, cols].bitcast(FP8X4), x_scales[:, cols], rounded)
 
         def quantise_wu(a):
-            rounded = ring.tile([P, PASS * PACK], BF16, name="wu_rounded", align_bytes=64, bufs=2)
+            rounded = keep.tile([P, PASS * PACK], BF16, name="wu_rounded", tag=f"wu_rounded{a}", align_bytes=64)
             for u in range(2):
                 nc.scalar.activation(
                     rounded[:].rearrange("p (t m i) -> p m i t", t=PACK, i=PACK)[:, u * (P // 2) : (u + 1) * (P // 2)],
@@ -133,9 +148,13 @@ def tile_list_relu_resP_kernel(tc, xT, wgt, wg_words, wg_scales, wu, wd_words, w
 
         def deal_scales():
             nc.vector.tensor_copy(
-                w_scales[:].rearrange("p (a t m) -> p a t m", a=HALVES, t=PACK),
-                scales_raw[:].rearrange("p (a m t) -> p a t m", a=HALVES, t=PACK),
+                w_scales[:].rearrange("p (t m) -> p t m", t=PACK),
+                scales_raw[:].rearrange("p (m t) -> p t m", t=PACK),
             )
+
+        def carry_scales():
+            for q in range(4):
+                nc.sync.dma_start(wd_late_scales[32 * q : 32 * q + 4, :].bitcast(I32), w_scales[32 * q + 4 : 32 * q + 8, :].bitcast(I32))
 
         def deal_wd():
             nc.vector.tensor_copy(
@@ -143,15 +162,17 @@ def tile_list_relu_resP_kernel(tc, xT, wgt, wg_words, wg_scales, wu, wd_words, w
                 wd_raw[:].bitcast(U16).rearrange("p (a m t) -> p a t m", a=HALVES, t=PACK),
             )
 
-        def hidden(a, c, rounded):
+        def hidden(a, c):
+            s, at = h_place(a, c)
+            rounded = h_rounded[s][:, at * PACK : (at + CHUNK) * PACK]
             cols = slice(c * CHUNK, (c + 1) * CHUNK)
-            gate = psum.tile([P, PACK, CHUNK], F32, name="gate", bufs=3)
+            gate = psum.tile([P, PACK, CHUNK], F32, name="gate", tag="gate", bufs=3)
             up = psum.tile([P, PACK, CHUNK], F32, name="up", bufs=3)
             for t in range(PACK):
                 nc.tensor.matmul_mx(
                     gate[:, t, :],
                     lhsT=wg_codes[a][:, t * P : (t + 1) * P].bitcast(FP8X4),
-                    lhsT_scale=w_scales[WG_ROW:P, a * PASS + t * P : a * PASS + (t + 1) * P],
+                    lhsT_scale=w_scales[WG_ROW + 4 * a : P, t * P : (t + 1) * P],
                     rhs=x_codes[:, cols].bitcast(FP8X4),
                     rhs_scale=x_scales[:, cols],
                     start=True,
@@ -176,81 +197,113 @@ def tile_list_relu_resP_kernel(tc, xT, wgt, wg_words, wg_scales, wu, wd_words, w
                 MULT,
             )
 
-        def hidden_group(a, c0, count):
-            rounded = ring.tile([P, count * CHUNK * PACK], BF16, name="h_rounded", align_bytes=64)
-            for c in range(count):
-                hidden(a, c0 + c, rounded[:, c * CHUNK * PACK : (c + 1) * CHUNK * PACK])
-            return rounded
-
-        def quantise_h(a, c0, count, rounded):
-            cols = slice(c0 * CHUNK, (c0 + count) * CHUNK)
-            nc.vector.quantize_mx(h_codes[a][:, cols].bitcast(FP8X4), h_scales[a][:, cols], rounded[:])
-            if a == HALVES - 1:
-                for c in range(c0, c0 + count):
-                    down(c)
+        def quantise_h(s, at, width):
+            cols = slice(at, at + width)
+            nc.vector.quantize_mx(h_codes[s][:, cols].bitcast(FP8X4), h_scales[s][:, cols], h_rounded[s][:, at * PACK : (at + width) * PACK])
 
         starts = [sum(OUT_WIDTHS[:u]) for u in range(len(OUT_WIDTHS))]
         results = [keep.tile([P, PACK, w], F32, name=f"result{u}") for u, w in enumerate(OUT_WIDTHS)]
 
         def down(c):
-            cols = slice(c * CHUNK, (c + 1) * CHUNK)
-            y = psum.tile([P, PACK, CHUNK], F32, name="y", bufs=2)
+            late = c >= CHUNKS - 2
+            y = psum.tile([P, PACK, CHUNK], F32, name="y", tag="gate" if late else "y", bufs=3 if late else 2)
             for a in range(HALVES):
+                s, at = h_place(a, c)
+                cols = slice(at, at + CHUNK)
                 for t in range(PACK):
                     nc.tensor.matmul_mx(
                         y[:, t, :],
                         lhsT=wd_codes[:, 2 * (a * PASS + t * P) : 2 * (a * PASS + (t + 1) * P)].bitcast(FP4X4),
-                        lhsT_scale=w_scales[:, a * PASS + t * P : a * PASS + (t + 1) * P],
-                        rhs=h_codes[a][:, cols].bitcast(FP8X4),
-                        rhs_scale=h_scales[a][:, cols],
+                        lhsT_scale=(w_scales, wd_late_scales)[a][:, t * P : (t + 1) * P],
+                        rhs=h_codes[s][:, cols].bitcast(FP8X4),
+                        rhs_scale=h_scales[s][:, cols],
                         start=(a == 0 and t == 0),
                         stop=(a == HALVES - 1 and t == PACK - 1),
                     )
+            return y
+
+        def add_res(c, y):
             u = max(v for v in range(len(starts)) if starts[v] <= c * CHUNK)
             at = c * CHUNK - starts[u]
             h, r0 = divmod(c * CHUNK, J // 2)
-            nc.vector.tensor_tensor(results[u][:, :, at : at + CHUNK], y[:], res_tiles[h][:, :, r0 : r0 + CHUNK], ADD)
+            if c in GPSIMD_CHUNKS:
+                staged = ring.tile([P, PACK, CHUNK], F32, name="y_staged", bufs=2)
+                nc.scalar.copy(staged[:], y[:])
+                nc.gpsimd.tensor_tensor(results[u][:, :, at : at + CHUNK], staged[:], res_tiles[h][:, :, r0 : r0 + CHUNK], ADD)
+            else:
+                parts = 1
+                w = CHUNK // parts
+                for v in range(parts):
+                    nc.vector.tensor_tensor(
+                        results[u][:, :, at + v * w : at + (v + 1) * w],
+                        y[:, :, v * w : (v + 1) * w],
+                        res_tiles[h][:, :, r0 + v * w : r0 + (v + 1) * w],
+                        ADD,
+                    )
             if at + CHUNK == OUT_WIDTHS[u]:
-                hand_out(u)
+                round_out(u)
 
-        def hand_out(u):
+        out_rounded = [keep.tile([P, w * PACK], BF16, name=f"out_rounded{u}", align_bytes=64) for u, w in enumerate(OUT_WIDTHS)]
+
+        def round_out(u):
             cols = slice(starts[u], starts[u] + OUT_WIDTHS[u])
             nc.sync.dma_start(out_rows[:, :, cols], results[u][:])
-            rounded = keep.tile([P, OUT_WIDTHS[u] * PACK], BF16, name=f"out_rounded{u}", align_bytes=64)
-            interleave(rounded[:], results[u][:], nc.vector.tensor_copy if u == len(OUT_WIDTHS) - 1 else nc.scalar.copy)
-            nc.vector.quantize_mx(out_codes[:, cols].bitcast(FP8X4), out_scales[:, cols], rounded[:])
+            interleave(out_rounded[u][:], results[u][:], nc.vector.tensor_copy if u == len(OUT_WIDTHS) - 1 else nc.scalar.copy)
+
+        def quantise_out(u):
+            cols = slice(starts[u], starts[u] + OUT_WIDTHS[u])
+            nc.vector.quantize_mx(out_codes[:, cols].bitcast(FP8X4), out_scales[:, cols], out_rounded[u][:])
             end = cols.stop
             if end % SLICE == 0:
                 nc.sync.dma_start(out_words[:, end - SLICE : end], out_codes[:, end - SLICE : end].bitcast(I32))
 
         gather(0, 0, SLICE)
-        gather(0, SLICE, SLICE)
-        gather(0, J // 2, J // 2)
+        gather(0, SLICE, J - SLICE)
         for i in range(1, PACK - 1):
-            for s in range(2):
-                gather(i, s * (J // 2), J // 2)
-        for s in range(SLICES):
-            gather(PACK - 1, s * SLICE, SLICE)
-        quantise_wu(0)
-        quantise_x(0, SLICE)
+            gather(i, 0, J)
+        for j0, width in ((0, CHUNK), (CHUNK, 3 * CHUNK), (J // 2, J // 2)):
+            gather(PACK - 1, j0, width)
+        quantise_x(0, CHUNK)
         deal_scales()
         deal_wg(0)
+        quantise_wu(0)
+        quantise_x(CHUNK, CHUNK)
 
-        groups = [(0, 0, 2), (0, 2, 2), (1, 0, 2), (0, 4, 2), (1, 2, 2), (0, 6, 2), (1, 4, 2), (1, 6, 1), (1, 7, 1)]
-        waiting = None
-        for n, (a, c0, count) in enumerate(groups):
-            if a == 0 and c0 > 0:
-                quantise_x(c0 * CHUNK, SLICE)
-            if n == 1:
-                deal_wd()
-            if (a, c0) == (1, 0):
-                quantise_wu(1)
-                deal_wg(1)
-            rounded = hidden_group(a, c0, count)
-            if waiting is not None:
-                quantise_h(*waiting)
-            waiting = (a, c0, count, rounded)
-        quantise_h(*waiting)
+        hidden(0, 0)
+        hidden(0, 1)
+        quantise_x(SLICE, SLICE)
+        deal_wg(1)
+        deal_wd()
+        carry_scales()
+        quantise_wu(1)
+        hidden(1, 0)
+        hidden(1, 1)
+        for s in range(1, SLICES):
+            c = 2 * s
+            hidden(0, c)
+            quantise_h(s - 1, 0, HALVES * SLICE)
+            if s > 1:
+                quantise_out(s - 2)
+            sums = [down(c - 2), down(c - 1)]
+            if s + 1 < SLICES:
+                quantise_x((s + 1) * SLICE, SLICE)
+            hidden(0, c + 1)
+            add_res(c - 2, sums[0])
+            hidden(1, c)
+            add_res(c - 1, sums[1])
+            if s + 1 == SLICES:
+                quantise_h(s, 0, SLICE)
+            hidden(1, c + 1)
+        last = SLICES - 1
+        quantise_h(last, SLICE, CHUNK)
+        sums = [down(CHUNKS - 2)]
+        quantise_out(last - 1)
+        quantise_h(last, SLICE + CHUNK, CHUNK)
+        sums.append(down(CHUNKS - 1))
+        add_res(CHUNKS - 2, sums[0])
+        add_res(CHUNKS - 1, sums[1])
+        quantise_out(last)
+        quantise_out(last + 1)
 
         queues = (nc.sync, nc.scalar, nc.sync, nc.scalar)
         for q in range(4):

@@ -1,6 +1,7 @@
 from contextlib import ExitStack
 
 import concourse.mybir as mybir
+from concourse.masks import make_identity
 
 K, R, N, T, J = 512, 1024, 512, 2048, 1024
 FLOPS = 2 * K * R * J * 2 + 2 * R * N * J
@@ -53,18 +54,23 @@ def tile_list_relu_resP_kernel(tc, xT, wgt, wg_words, wg_scales, wu, wd_words, w
         wd_raw = keep.tile([P, HALVES * N * 2], U8, name="wd_raw")
         scales_raw = keep.tile([P, PASS], U8, name="scales_raw")
         wd_late_scales = keep.tile([P, PASS], U8, name="wd_late_scales", align_bytes=64)
-        res_tiles = [keep.tile([P, PACK, J // 2], F32, name=f"res{h}") for h in range(2)]
+        res_tiles = [keep.tile([P, PACK, SLICE], F32, name=f"res{s}") for s in range(SLICES)]
         res_rows = res.rearrange("(p t) j -> p t j", t=PACK)
         out_rows = out_0.rearrange("(p t) j -> p t j", t=PACK)
         out_words = out_1[0].rearrange("p j i -> p (j i)").bitcast(I32)
 
-        nc.gpsimd.memset(scales_raw[:].bitcast(I32), 0)
+        head_rows = keep.tile([P, P], F32, name="head_rows")
+        identity = keep.tile([P, P], F32, name="identity")
+        nc.sync.dma_start(head_rows[0:32, :], wgt[:, J // 2 : J].rearrange("(g v) (u e) -> v g u e", v=16, e=P)[0])
+        nc.vector.memset(head_rows[32:64, :], 0.0)
+        nc.vector.memset(head_rows[64:P, :], 0.0)
+        nc.vector.memset(scales_raw[:].bitcast(I32), 0)
+        make_identity(nc, identity[:])
         nc.gpsimd.memset(wd_late_scales[:].bitcast(I32), 0)
 
         nc.sync.dma_start(x_planes[0][:], x_rows[0])
         nc.sync.dma_start(offsets[:], offs)
-        nc.sync.dma_start(weights[:, 0:SLICE], wgt[:, 0:SLICE])
-        nc.sync.dma_start(weights[:, SLICE:J], wgt[:, SLICE:J])
+        nc.sync.dma_start(weights[:, 0 : J // 2], wgt[:, 0 : J // 2])
         nc.sync.dma_start(x_planes[1][:], x_rows[1])
         for q in range(4):
             nc.sync.dma_start(
@@ -85,8 +91,7 @@ def tile_list_relu_resP_kernel(tc, xT, wgt, wg_words, wg_scales, wu, wd_words, w
             nc.sync.dma_start(wu_raw[u][:], wu_rows[:, :, u * WU_PIECE : (u + 1) * WU_PIECE])
         nc.sync.dma_start(wg_raw[1][:], wg_rows[:, PASS:R])
         nc.sync.dma_start(wd_raw[:].bitcast(I32).rearrange("p (a w) -> p a w", a=HALVES), wd_words.bitcast(I32).rearrange("a p w -> p a w"))
-        for h in range(2):
-            nc.sync.dma_start(res_tiles[h][:], res_rows[:, :, h * (J // 2) : (h + 1) * (J // 2)])
+        nc.sync.dma_start(res_tiles[0][:], res_rows[:, :, 0:SLICE])
 
         picked = [keep.tile([P, PACK, w], F32, name=f"picked{s}", align_bytes=64) for s, w in enumerate(PICK_WIDTHS)]
         pick_starts = [sum(PICK_WIDTHS[:s]) for s in range(len(PICK_WIDTHS))]
@@ -102,7 +107,7 @@ def tile_list_relu_resP_kernel(tc, xT, wgt, wg_words, wg_scales, wu, wd_words, w
         wg_codes = [keep.tile([P, PASS], I32, name=f"wg_codes{a}", align_bytes=64) for a in range(HALVES)]
         wd_codes = keep.tile([P, HALVES * N * 2], U8, name="wd_codes", align_bytes=64)
         w_scales = keep.tile([P, PASS], U8, name="w_scales", align_bytes=64)
-        h_rounded = [keep.tile([P, HALVES * SLICE * PACK], BF16, name=f"h_rounded{s}", align_bytes=64) for s in range(SLICES)]
+        h_rounded = [keep.tile([P, HALVES * SLICE * PACK], BF16, name=f"h_rounded{s}", tag=f"h_rounded{s}", align_bytes=64) for s in range(SLICES)]
         h_codes = [keep.tile([P, HALVES * SLICE], U32, name=f"h_codes{s}", align_bytes=64) for s in range(SLICES)]
         h_scales = [keep.tile([P, HALVES * SLICE], U8, name=f"h_scales{s}", align_bytes=64) for s in range(SLICES)]
 
@@ -123,12 +128,19 @@ def tile_list_relu_resP_kernel(tc, xT, wgt, wg_words, wg_scales, wu, wd_words, w
                 planes.rearrange("p t (c e) -> p c t e", e=4),
             )
 
-        def quantise_x(j0, width):
+        x_rounded = {}
+
+        def round_x(j0, width):
             s, at = place(j0)
             rounded = keep.tile([P, width * PACK], BF16, name="x_rounded", tag=X_ROUNDED_IN[j0], align_bytes=64)[:]
             interleave(rounded, picked[s][:, :, at : at + width], nc.vector.tensor_copy if j0 == SLICE else nc.scalar.copy)
+            x_rounded[j0] = rounded
+
+        def quantise_x(j0, width):
+            if j0 not in x_rounded:
+                round_x(j0, width)
             cols = slice(j0, j0 + width)
-            nc.vector.quantize_mx(x_codes[:, cols].bitcast(FP8X4), x_scales[:, cols], rounded)
+            nc.vector.quantize_mx(x_codes[:, cols].bitcast(FP8X4), x_scales[:, cols], x_rounded[j0])
 
         def quantise_wu(a):
             rounded = keep.tile([P, PASS * PACK], BF16, name="wu_rounded", tag=f"wu_rounded{a}", align_bytes=64)
@@ -202,7 +214,7 @@ def tile_list_relu_resP_kernel(tc, xT, wgt, wg_words, wg_scales, wu, wd_words, w
             nc.vector.quantize_mx(h_codes[s][:, cols].bitcast(FP8X4), h_scales[s][:, cols], h_rounded[s][:, at * PACK : (at + width) * PACK])
 
         starts = [sum(OUT_WIDTHS[:u]) for u in range(len(OUT_WIDTHS))]
-        results = [keep.tile([P, PACK, w], F32, name=f"result{u}") for u, w in enumerate(OUT_WIDTHS)]
+        results = {u: keep.tile([P, PACK, w], F32, name=f"result{u}") for u, w in enumerate(OUT_WIDTHS) if u != 3}
 
         def down(c):
             late = c >= CHUNKS - 2
@@ -225,7 +237,7 @@ def tile_list_relu_resP_kernel(tc, xT, wgt, wg_words, wg_scales, wu, wd_words, w
         def add_res(c, y):
             u = max(v for v in range(len(starts)) if starts[v] <= c * CHUNK)
             at = c * CHUNK - starts[u]
-            h, r0 = divmod(c * CHUNK, J // 2)
+            h, r0 = divmod(c * CHUNK, SLICE)
             if c in GPSIMD_CHUNKS:
                 staged = ring.tile([P, PACK, CHUNK], F32, name="y_staged", bufs=2)
                 nc.scalar.copy(staged[:], y[:])
@@ -257,24 +269,36 @@ def tile_list_relu_resP_kernel(tc, xT, wgt, wg_words, wg_scales, wu, wd_words, w
             if end % SLICE == 0:
                 nc.sync.dma_start(out_words[:, end - SLICE : end], out_codes[:, end - SLICE : end].bitcast(I32))
 
-        gather(0, 0, SLICE)
-        gather(0, SLICE, J - SLICE)
+        turned = psum.tile([P, P], F32, name="turned", tag="y", bufs=2)
+        nc.tensor.transpose(turned[:], head_rows[:], identity[:])
+        spread = keep.tile([P, PACK, 8, 16], F32, name="spread")
+        nc.scalar.copy(spread[:], turned[:, 0:32].rearrange("e (g u) -> e u g", u=PACK).unsqueeze(3).to_broadcast([P, PACK, 8, 16]))
+        back = psum.tile([P, PACK, P], F32, name="back", tag="gate", bufs=3)
+        for u in range(PACK):
+            nc.tensor.transpose(back[:, u, :], spread[:, u].rearrange("e g v -> e (g v)"), identity[:])
+        nc.scalar.copy(weights[:, J // 2 : J], back[:].rearrange("p u e -> p (u e)"))
+
+        gather(0, 0, J // 2)
+        gather(0, J // 2, J // 2)
         for i in range(1, PACK - 1):
             gather(i, 0, J)
-        for j0, width in ((0, CHUNK), (CHUNK, 3 * CHUNK), (J // 2, J // 2)):
+        for j0, width in ((0, CHUNK), (CHUNK, J - CHUNK)):
             gather(PACK - 1, j0, width)
         quantise_x(0, CHUNK)
         deal_scales()
+        carry_scales()
+        for s in range(1, SLICES):
+            nc.sync.dma_start(res_tiles[s][:], res_rows[:, :, s * SLICE : (s + 1) * SLICE])
         deal_wg(0)
         quantise_wu(0)
         quantise_x(CHUNK, CHUNK)
 
         hidden(0, 0)
         hidden(0, 1)
-        quantise_x(SLICE, SLICE)
+        round_x(SLICE, SLICE)
         deal_wg(1)
+        quantise_x(SLICE, SLICE)
         deal_wd()
-        carry_scales()
         quantise_wu(1)
         hidden(1, 0)
         hidden(1, 1)
@@ -293,13 +317,14 @@ def tile_list_relu_resP_kernel(tc, xT, wgt, wg_words, wg_scales, wu, wd_words, w
             add_res(c - 1, sums[1])
             if s + 1 == SLICES:
                 quantise_h(s, 0, SLICE)
+                quantise_h(s, SLICE, CHUNK)
             hidden(1, c + 1)
         last = SLICES - 1
-        quantise_h(last, SLICE, CHUNK)
         sums = [down(CHUNKS - 2)]
         quantise_out(last - 1)
         quantise_h(last, SLICE + CHUNK, CHUNK)
         sums.append(down(CHUNKS - 1))
+        results[3] = keep.tile([P, PACK, CHUNK], F32, name="result3", tag=f"h_rounded{last}", align_bytes=64)
         add_res(CHUNKS - 2, sums[0])
         add_res(CHUNKS - 1, sums[1])
         quantise_out(last)

@@ -32,6 +32,7 @@ WU_PIECE = PASS // 2
 OUT_WIDTHS = (256, 256, 256, 128, 128)
 PICK_WIDTHS = (1024,)
 GPSIMD_CHUNKS = ()
+SPREAD_PARTS = (2, 3, 3)
 X_ROUNDED_IN = {0: "x_first", 128: "wu_raw1", 256: "wu_rounded0", 512: "wu_raw3", 768: "wu_raw3"}
 
 
@@ -61,8 +62,7 @@ def tile_list_relu_resP_kernel(tc, xT, wgt, wg_words, wg_scales, wu, wd_words, w
 
         head_rows = keep.tile([P, P], F32, name="head_rows")
         identity = keep.tile([P, P], F32, name="identity")
-        nc.sync.dma_start(head_rows[0:32, :], wgt[:, J // 2 : J].rearrange("(g v) (u e) -> v g u e", v=16, e=P)[0])
-        nc.vector.memset(head_rows[32:64, :], 0.0)
+        nc.sync.dma_start(head_rows[0:64, :], wgt.rearrange("(g v) (u e) -> v g u e", v=16, e=P)[0])
         nc.vector.memset(head_rows[64:P, :], 0.0)
         nc.vector.memset(scales_raw[:].bitcast(I32), 0)
         make_identity(nc, identity[:])
@@ -70,7 +70,6 @@ def tile_list_relu_resP_kernel(tc, xT, wgt, wg_words, wg_scales, wu, wd_words, w
 
         nc.sync.dma_start(x_planes[0][:], x_rows[0])
         nc.sync.dma_start(offsets[:], offs)
-        nc.sync.dma_start(weights[:, 0 : J // 2], wgt[:, 0 : J // 2])
         nc.sync.dma_start(x_planes[1][:], x_rows[1])
         for q in range(4):
             nc.sync.dma_start(
@@ -174,38 +173,46 @@ def tile_list_relu_resP_kernel(tc, xT, wgt, wg_words, wg_scales, wu, wd_words, w
                 wd_raw[:].bitcast(U16).rearrange("p (a m t) -> p a t m", a=HALVES, t=PACK),
             )
 
+        def product(out, codes, scales, cols):
+            nc.tensor.matmul_mx(out, lhsT=codes.bitcast(FP8X4), lhsT_scale=scales, rhs=x_codes[:, cols].bitcast(FP8X4), rhs_scale=x_scales[:, cols], start=True, stop=True)
+
+        ready = {}
+
+        def sums_of(a, c0, count):
+            width = count * CHUNK
+            ups = []
+
+            def up_sums():
+                for c in range(c0, c0 + count):
+                    up = psum.tile([P, PACK, CHUNK], F32, name="up", tag="up", bufs=3)
+                    for t in range(PACK):
+                        product(up[:, t, :], wu_codes[a][:, t * P : (t + 1) * P], wu_scales[a][:, t * P : (t + 1) * P], slice(c * CHUNK, (c + 1) * CHUNK))
+                    ups.append(up)
+
+            if c0 > 1:
+                up_sums()
+            opened = ring.tile([P, CHUNK // 2, PACK, 2], F32, name="opened", bufs=4)
+            per_bank = PACK // count
+            for bank in range(count):
+                gate = psum.tile([P, per_bank, width], F32, name="gate", tag="gate", bufs=3)
+                for v in range(per_bank):
+                    t = bank * per_bank + v
+                    product(gate[:, v, :], wg_codes[a][:, t * P : (t + 1) * P], w_scales[WG_ROW + 4 * a : P, t * P : (t + 1) * P], slice(c0 * CHUNK, c0 * CHUNK + width))
+                nc.scalar.activation(opened[:, 0 : width // 2, bank * per_bank : (bank + 1) * per_bank, :], gate[:].rearrange("p t (c e) -> p c t e", e=2), RELU)
+            if c0 <= 1:
+                up_sums()
+            for v in range(count):
+                ready[a, c0 + v] = (ups[v], opened[:, v * CHUNK // 2 : (v + 1) * CHUNK // 2])
+
         def hidden(a, c):
+            if (a, c) not in ready:
+                sums_of(a, c, 1)
+            up, opened = ready[a, c]
             s, at = h_place(a, c)
-            rounded = h_rounded[s][:, at * PACK : (at + CHUNK) * PACK]
-            cols = slice(c * CHUNK, (c + 1) * CHUNK)
-            gate = psum.tile([P, PACK, CHUNK], F32, name="gate", tag="gate", bufs=3)
-            up = psum.tile([P, PACK, CHUNK], F32, name="up", bufs=3)
-            for t in range(PACK):
-                nc.tensor.matmul_mx(
-                    gate[:, t, :],
-                    lhsT=wg_codes[a][:, t * P : (t + 1) * P].bitcast(FP8X4),
-                    lhsT_scale=w_scales[WG_ROW + 4 * a : P, t * P : (t + 1) * P],
-                    rhs=x_codes[:, cols].bitcast(FP8X4),
-                    rhs_scale=x_scales[:, cols],
-                    start=True,
-                    stop=True,
-                )
-            for t in range(PACK):
-                nc.tensor.matmul_mx(
-                    up[:, t, :],
-                    lhsT=wu_codes[a][:, t * P : (t + 1) * P].bitcast(FP8X4),
-                    lhsT_scale=wu_scales[a][:, t * P : (t + 1) * P],
-                    rhs=x_codes[:, cols].bitcast(FP8X4),
-                    rhs_scale=x_scales[:, cols],
-                    start=True,
-                    stop=True,
-                )
-            opened = ring.tile([P, CHUNK // 2, PACK, 2], F32, name="opened")
-            nc.scalar.activation(opened[:], gate[:].rearrange("p t (c e) -> p c t e", e=2), RELU)
             nc.vector.tensor_tensor(
-                rounded.rearrange("p (c e t) -> p c t e", e=2, t=PACK),
+                h_rounded[s][:, at * PACK : (at + CHUNK) * PACK].rearrange("p (c e t) -> p c t e", e=2, t=PACK),
                 up[:].rearrange("p t (c e) -> p c t e", e=2),
-                opened[:],
+                opened,
                 MULT,
             )
 
@@ -271,15 +278,16 @@ def tile_list_relu_resP_kernel(tc, xT, wgt, wg_words, wg_scales, wu, wd_words, w
 
         turned = psum.tile([P, P], F32, name="turned", tag="y", bufs=2)
         nc.tensor.transpose(turned[:], head_rows[:], identity[:])
-        spread = keep.tile([P, PACK, 8, 16], F32, name="spread")
-        nc.scalar.copy(spread[:], turned[:, 0:32].rearrange("e (g u) -> e u g", u=PACK).unsqueeze(3).to_broadcast([P, PACK, 8, 16]))
-        back = psum.tile([P, PACK, P], F32, name="back", tag="gate", bufs=3)
-        for u in range(PACK):
-            nc.tensor.transpose(back[:, u, :], spread[:, u].rearrange("e g v -> e (g v)"), identity[:])
-        nc.scalar.copy(weights[:, J // 2 : J], back[:].rearrange("p u e -> p (u e)"))
-
-        gather(0, 0, J // 2)
-        gather(0, J // 2, J // 2)
+        u0 = 0
+        for part, count in enumerate(SPREAD_PARTS):
+            spread = keep.tile([P, count, 8, 16], F32, name=f"spread{part}")
+            nc.scalar.copy(spread[:], turned[:, 0:64].rearrange("e (g u) -> e u g", u=8)[:, u0 : u0 + count, :].unsqueeze(3).to_broadcast([P, count, 8, 16]))
+            back = psum.tile([P, count, P], F32, name="back", tag="gate", bufs=3)
+            for u in range(count):
+                nc.tensor.transpose(back[:, u, :], spread[:, u].rearrange("e g v -> e (g v)"), identity[:])
+            nc.scalar.copy(weights[:, u0 * P : (u0 + count) * P], back[:].rearrange("p u e -> p (u e)"))
+            gather(0, u0 * P, count * P)
+            u0 = u0 + count
         for i in range(1, PACK - 1):
             gather(i, 0, J)
         for j0, width in ((0, CHUNK), (CHUNK, J - CHUNK)):

@@ -30,8 +30,10 @@ SLICES = J // SLICE
 WG_ROW = 8
 WU_PIECE = PASS // 2
 OUT_WIDTHS = (256, 256, 256, 128, 128)
+SPLIT_SLICES = 2
+H_CODES_IN = ("h_codes0", "wu_raw3", "out_rounded0", "y_staged2")
 PICK_WIDTHS = (1024,)
-GPSIMD_CHUNKS = ()
+GPSIMD_CHUNKS = (0, 2)
 SPREAD_PARTS = (2, 3, 3)
 X_ROUNDED_IN = {0: "x_first", 128: "wu_raw1", 256: "wu_rounded0", 512: "wu_raw3", 768: "wu_raw3"}
 
@@ -107,7 +109,7 @@ def tile_list_relu_resP_kernel(tc, xT, wgt, wg_words, wg_scales, wu, wd_words, w
         wd_codes = keep.tile([P, HALVES * N * 2], U8, name="wd_codes", align_bytes=64)
         w_scales = keep.tile([P, PASS], U8, name="w_scales", align_bytes=64)
         h_rounded = [keep.tile([P, HALVES * SLICE * PACK], BF16, name=f"h_rounded{s}", tag=f"h_rounded{s}", align_bytes=64) for s in range(SLICES)]
-        h_codes = [keep.tile([P, HALVES * SLICE], U32, name=f"h_codes{s}", align_bytes=64) for s in range(SLICES)]
+        h_codes = {}
         h_scales = [keep.tile([P, HALVES * SLICE], U8, name=f"h_scales{s}", align_bytes=64) for s in range(SLICES)]
 
         def h_place(a, c):
@@ -218,10 +220,12 @@ def tile_list_relu_resP_kernel(tc, xT, wgt, wg_words, wg_scales, wu, wd_words, w
 
         def quantise_h(s, at, width):
             cols = slice(at, at + width)
+            if s not in h_codes:
+                h_codes[s] = keep.tile([P, HALVES * SLICE], U32, name="h_codes", tag=H_CODES_IN[s], align_bytes=64)
             nc.vector.quantize_mx(h_codes[s][:, cols].bitcast(FP8X4), h_scales[s][:, cols], h_rounded[s][:, at * PACK : (at + width) * PACK])
 
         starts = [sum(OUT_WIDTHS[:u]) for u in range(len(OUT_WIDTHS))]
-        results = {u: keep.tile([P, PACK, w], F32, name=f"result{u}") for u, w in enumerate(OUT_WIDTHS) if u != 3}
+        results = {u: keep.tile([P, PACK, w], F32, name=f"result{u}") for u, w in enumerate(OUT_WIDTHS) if u in (2, 4)}
 
         def down(c):
             late = c >= CHUNKS - 2
@@ -241,28 +245,36 @@ def tile_list_relu_resP_kernel(tc, xT, wgt, wg_words, wg_scales, wu, wd_words, w
                     )
             return y
 
+        staged = {}
+
+        def finish_chunk(c, result):
+            u, half = divmod(c, 2)
+            nc.sync.dma_start(out_rows[:, :, c * CHUNK : (c + 1) * CHUNK], result[:])
+            interleave(out_rounded[u][:, half * CHUNK * PACK : (half + 1) * CHUNK * PACK], result[:])
+
+        def add_staged(c):
+            h, r0 = divmod(c * CHUNK, SLICE)
+            result = keep.tile([P, PACK, CHUNK], F32, name="result_late", tag=f"h_rounded{h + 1}", align_bytes=64)
+            nc.gpsimd.tensor_tensor(result[:], staged[c][:], res_tiles[h][:, :, r0 : r0 + CHUNK], ADD)
+            finish_chunk(c, result)
+
         def add_res(c, y):
             u = max(v for v in range(len(starts)) if starts[v] <= c * CHUNK)
             at = c * CHUNK - starts[u]
             h, r0 = divmod(c * CHUNK, SLICE)
             if c in GPSIMD_CHUNKS:
-                staged = ring.tile([P, PACK, CHUNK], F32, name="y_staged", bufs=2)
-                nc.scalar.copy(staged[:], y[:])
-                nc.gpsimd.tensor_tensor(results[u][:, :, at : at + CHUNK], staged[:], res_tiles[h][:, :, r0 : r0 + CHUNK], ADD)
+                staged[c] = keep.tile([P, PACK, CHUNK], F32, name=f"y_staged{c}", tag=f"y_staged{c}", align_bytes=64)
+                nc.scalar.copy(staged[c][:], y[:])
+            elif u < SPLIT_SLICES:
+                result = keep.tile([P, PACK, CHUNK], F32, name=f"result_odd{c}")
+                nc.vector.tensor_tensor(result[:], y[:], res_tiles[h][:, :, r0 : r0 + CHUNK], ADD)
+                finish_chunk(c, result)
             else:
-                parts = 1
-                w = CHUNK // parts
-                for v in range(parts):
-                    nc.vector.tensor_tensor(
-                        results[u][:, :, at + v * w : at + (v + 1) * w],
-                        y[:, :, v * w : (v + 1) * w],
-                        res_tiles[h][:, :, r0 + v * w : r0 + (v + 1) * w],
-                        ADD,
-                    )
-            if at + CHUNK == OUT_WIDTHS[u]:
-                round_out(u)
+                nc.vector.tensor_tensor(results[u][:, :, at : at + CHUNK], y[:], res_tiles[h][:, :, r0 : r0 + CHUNK], ADD)
+                if at + CHUNK == OUT_WIDTHS[u]:
+                    round_out(u)
 
-        out_rounded = [keep.tile([P, w * PACK], BF16, name=f"out_rounded{u}", align_bytes=64) for u, w in enumerate(OUT_WIDTHS)]
+        out_rounded = [keep.tile([P, w * PACK], BF16, name=f"out_rounded{u}", tag=f"out_rounded{u}", align_bytes=64) for u, w in enumerate(OUT_WIDTHS)]
 
         def round_out(u):
             cols = slice(starts[u], starts[u] + OUT_WIDTHS[u])
@@ -312,13 +324,15 @@ def tile_list_relu_resP_kernel(tc, xT, wgt, wg_words, wg_scales, wu, wd_words, w
         hidden(1, 1)
         for s in range(1, SLICES):
             c = 2 * s
+            if s + 1 < SLICES:
+                quantise_x((s + 1) * SLICE, SLICE)
+            else:
+                quantise_out(0)
             hidden(0, c)
             quantise_h(s - 1, 0, HALVES * SLICE)
             if s > 1:
-                quantise_out(s - 2)
+                add_staged(c - 4)
             sums = [down(c - 2), down(c - 1)]
-            if s + 1 < SLICES:
-                quantise_x((s + 1) * SLICE, SLICE)
             hidden(0, c + 1)
             add_res(c - 2, sums[0])
             hidden(1, c)
@@ -329,8 +343,9 @@ def tile_list_relu_resP_kernel(tc, xT, wgt, wg_words, wg_scales, wu, wd_words, w
             hidden(1, c + 1)
         last = SLICES - 1
         sums = [down(CHUNKS - 2)]
-        quantise_out(last - 1)
+        quantise_out(last - 2)
         quantise_h(last, SLICE + CHUNK, CHUNK)
+        quantise_out(last - 1)
         sums.append(down(CHUNKS - 1))
         results[3] = keep.tile([P, PACK, CHUNK], F32, name="result3", tag=f"h_rounded{last}", align_bytes=64)
         add_res(CHUNKS - 2, sums[0])

@@ -31,7 +31,7 @@ WG_ROW = 8
 WU_PIECE = PASS // 2
 OUT_WIDTHS = (256, 256, 256, 128, 128)
 SPLIT_SLICES = 2
-H_CODES_IN = ("h_codes0", "wu_raw3", "out_rounded0", "y_staged2")
+H_CODES_IN = ("h_codes0", "wu_raw3", "h_codes2", "y_staged2")
 PICK_WIDTHS = (1024,)
 GPSIMD_CHUNKS = (0, 2)
 SPREAD_PARTS = (2, 3, 3)
@@ -57,7 +57,7 @@ def tile_list_relu_resP_kernel(tc, xT, wgt, wg_words, wg_scales, wu, wd_words, w
         wd_raw = keep.tile([P, HALVES * N * 2], U8, name="wd_raw")
         scales_raw = keep.tile([P, PASS], U8, name="scales_raw")
         wd_late_scales = keep.tile([P, PASS], U8, name="wd_late_scales", align_bytes=64)
-        res_tiles = [keep.tile([P, PACK, SLICE], F32, name=f"res{s}") for s in range(SLICES)]
+        res_tiles = [keep.tile([P, PACK, SLICE], F32, name=f"res{s}", tag=f"res{s}", align_bytes=64) for s in range(SLICES)]
         res_rows = res.rearrange("(p t) j -> p t j", t=PACK)
         out_rows = out_0.rearrange("(p t) j -> p t j", t=PACK)
         out_words = out_1[0].rearrange("p j i -> p (j i)").bitcast(I32)
@@ -247,10 +247,15 @@ def tile_list_relu_resP_kernel(tc, xT, wgt, wg_words, wg_scales, wu, wd_words, w
 
         staged = {}
 
+        chunk_results = {}
+
         def finish_chunk(c, result):
-            u, half = divmod(c, 2)
             nc.sync.dma_start(out_rows[:, :, c * CHUNK : (c + 1) * CHUNK], result[:])
-            interleave(out_rounded[u][:, half * CHUNK * PACK : (half + 1) * CHUNK * PACK], result[:])
+            chunk_results[c] = result
+
+        def round_chunk(c):
+            u, half = divmod(c, 2)
+            interleave(out_rounded[u][:, half * CHUNK * PACK : (half + 1) * CHUNK * PACK], chunk_results[c][:])
 
         def add_staged(c):
             h, r0 = divmod(c * CHUNK, SLICE)
@@ -283,8 +288,13 @@ def tile_list_relu_resP_kernel(tc, xT, wgt, wg_words, wg_scales, wu, wd_words, w
 
         def quantise_out(u):
             cols = slice(starts[u], starts[u] + OUT_WIDTHS[u])
-            nc.vector.quantize_mx(out_codes[:, cols].bitcast(FP8X4), out_scales[:, cols], out_rounded[u][:])
             end = cols.stop
+            if u == 0:
+                first_codes = keep.tile([P, SLICE], U32, name="first_codes", tag="res1", align_bytes=64)
+                nc.vector.quantize_mx(first_codes[:].bitcast(FP8X4), out_scales[:, cols], out_rounded[u][:])
+                nc.sync.dma_start(out_words[:, cols], first_codes[:].bitcast(I32))
+                return
+            nc.vector.quantize_mx(out_codes[:, cols].bitcast(FP8X4), out_scales[:, cols], out_rounded[u][:])
             if end % SLICE == 0:
                 nc.sync.dma_start(out_words[:, end - SLICE : end], out_codes[:, end - SLICE : end].bitcast(I32))
 
@@ -326,8 +336,6 @@ def tile_list_relu_resP_kernel(tc, xT, wgt, wg_words, wg_scales, wu, wd_words, w
             c = 2 * s
             if s + 1 < SLICES:
                 quantise_x((s + 1) * SLICE, SLICE)
-            else:
-                quantise_out(0)
             hidden(0, c)
             quantise_h(s - 1, 0, HALVES * SLICE)
             if s > 1:
@@ -337,7 +345,11 @@ def tile_list_relu_resP_kernel(tc, xT, wgt, wg_words, wg_scales, wu, wd_words, w
             add_res(c - 2, sums[0])
             hidden(1, c)
             add_res(c - 1, sums[1])
+            if s > 1:
+                round_chunk(c - 3)
+                round_chunk(c - 4)
             if s + 1 == SLICES:
+                quantise_out(0)
                 quantise_h(s, 0, SLICE)
                 quantise_h(s, SLICE, CHUNK)
             hidden(1, c + 1)

@@ -88,9 +88,9 @@ def tile_list_relu_resP_kernel(tc, xT, wgt, wg_words, wg_scales, wu, wd_words, w
         for u in range(2):
             nc.sync.dma_start(wu_raw[u][:], wu_rows[:, :, u * WU_PIECE : (u + 1) * WU_PIECE])
         nc.sync.dma_start(wg_raw[0][:], wg_rows[:, 0:PASS])
+        nc.sync.dma_start(wg_raw[1][:], wg_rows[:, PASS:R])
         for u in range(2, 4):
             nc.sync.dma_start(wu_raw[u][:], wu_rows[:, :, u * WU_PIECE : (u + 1) * WU_PIECE])
-        nc.sync.dma_start(wg_raw[1][:], wg_rows[:, PASS:R])
         nc.sync.dma_start(wd_raw[:].bitcast(I32).rearrange("p (a w) -> p a w", a=HALVES), wd_words.bitcast(I32).rearrange("a p w -> p a w"))
         nc.sync.dma_start(res_tiles[0][:], res_rows[:, :, 0:SLICE])
 
@@ -321,12 +321,12 @@ def tile_list_relu_resP_kernel(tc, xT, wgt, wg_words, wg_scales, wu, wd_words, w
             nc.sync.dma_start(res_tiles[s][:], res_rows[:, :, s * SLICE : (s + 1) * SLICE])
         deal_wg(0)
         quantise_wu(0)
+        deal_wg(1)
         quantise_x(CHUNK, CHUNK)
 
         hidden(0, 0)
         hidden(0, 1)
         round_x(SLICE, SLICE)
-        deal_wg(1)
         quantise_x(SLICE, SLICE)
         deal_wd()
         quantise_wu(1)

@@ -186,7 +186,8 @@ def tile_list_relu_resP_kernel(tc, xT, wgt, wg_words, wg_scales, wu, wd_words, w
 
             def up_sums():
                 for c in range(c0, c0 + count):
-                    up = psum.tile([P, PACK, CHUNK], F32, name="up", tag="up", bufs=3)
+                    final = (a, c) == (HALVES - 1, CHUNKS - 1)
+                    up = psum.tile([P, PACK, CHUNK], F32, name="up", tag="y" if final else "up", bufs=2 if final else 3)
                     for t in range(PACK):
                         product(up[:, t, :], wu_codes[a][:, t * P : (t + 1) * P], wu_scales[a][:, t * P : (t + 1) * P], slice(c * CHUNK, (c + 1) * CHUNK))
                     ups.append(up)
@@ -307,7 +308,7 @@ def tile_list_relu_resP_kernel(tc, xT, wgt, wg_words, wg_scales, wu, wd_words, w
             back = psum.tile([P, count, P], F32, name="back", tag="gate", bufs=3)
             for u in range(count):
                 nc.tensor.transpose(back[:, u, :], spread[:, u].rearrange("e g v -> e (g v)"), identity[:])
-            nc.scalar.copy(weights[:, u0 * P : (u0 + count) * P], back[:].rearrange("p u e -> p (u e)"))
+            (nc.vector.tensor_copy if part == 0 else nc.scalar.copy)(weights[:, u0 * P : (u0 + count) * P], back[:].rearrange("p u e -> p (u e)"))
             gather(0, u0 * P, count * P)
             u0 = u0 + count
         for i in range(1, PACK - 1):

@@ -350,19 +350,18 @@ def tile_list_relu_resP_kernel(tc, xT, wgt, wg_words, wg_scales, wu, wd_words, w
                 round_chunk(c - 3)
                 round_chunk(c - 4)
             if s + 1 == SLICES:
-                quantise_out(0)
-                quantise_h(s, 0, SLICE)
-                quantise_h(s, SLICE, CHUNK)
+                quantise_h(s, 0, SLICE + CHUNK)
             hidden(1, c + 1)
         last = SLICES - 1
         sums = [down(CHUNKS - 2)]
-        quantise_out(last - 2)
+        quantise_out(0)
         quantise_h(last, SLICE + CHUNK, CHUNK)
-        quantise_out(last - 1)
         sums.append(down(CHUNKS - 1))
         results[3] = keep.tile([P, PACK, CHUNK], F32, name="result3", tag=f"h_rounded{last}", align_bytes=64)
         add_res(CHUNKS - 2, sums[0])
+        quantise_out(last - 2)
         add_res(CHUNKS - 1, sums[1])
+        quantise_out(last - 1)
         quantise_out(last)
         quantise_out(last + 1)
 

@@ -50,14 +50,14 @@ def tile_list_relu_resP_kernel(tc, xT, wgt, wg_words, wg_scales, wu, wd_words, w
         weights = keep.tile([P, J], F32, name="weights")
         x_planes = [keep.tile([P, T], F32, name=f"x_plane{i}") for i in range(PACK)]
         x_rows = xT.rearrange("(p i) t -> i p t", i=PACK)
-        wu_raw = [keep.tile([P, PACK, WU_PIECE], F32, name=f"wu_raw{u}", tag=f"wu_raw{u}", align_bytes=64) for u in range(R // WU_PIECE)]
+        wu_raw = [keep.tile([P, PACK, WU_PIECE], F32, name=f"wu_raw{u}", tag=f"wu_raw{u}", align_bytes=256) for u in range(R // WU_PIECE)]
         wu_rows = wu.rearrange("(p i) r -> p i r", i=PACK)
         wg_raw = [keep.tile([P, PASS], I32, name=f"wg_raw{a}") for a in range(HALVES)]
         wg_rows = wg_words[0].rearrange("p r i -> p (r i)").bitcast(I32)
         wd_raw = keep.tile([P, HALVES * N * 2], U8, name="wd_raw")
         scales_raw = keep.tile([P, PASS], U8, name="scales_raw")
-        wd_late_scales = keep.tile([P, PASS], U8, name="wd_late_scales", align_bytes=64)
-        res_tiles = [keep.tile([P, PACK, SLICE], F32, name=f"res{s}", tag=f"res{s}", align_bytes=64) for s in range(SLICES)]
+        wd_late_scales = keep.tile([P, PASS], U8, name="wd_late_scales", align_bytes=256)
+        res_tiles = [keep.tile([P, PACK, SLICE], F32, name=f"res{s}", tag=f"res{s}", align_bytes=256) for s in range(SLICES)]
         res_rows = res.rearrange("(p t) j -> p t j", t=PACK)
         out_rows = out_0.rearrange("(p t) j -> p t j", t=PACK)
         out_words = out_1[0].rearrange("p j i -> p (j i)").bitcast(I32)
@@ -94,29 +94,29 @@ def tile_list_relu_resP_kernel(tc, xT, wgt, wg_words, wg_scales, wu, wd_words, w
         nc.sync.dma_start(wd_raw[:].bitcast(I32).rearrange("p (a w) -> p a w", a=HALVES), wd_words.bitcast(I32).rearrange("a p w -> p a w"))
         nc.sync.dma_start(res_tiles[0][:], res_rows[:, :, 0:SLICE])
 
-        picked = [keep.tile([P, PACK, w], F32, name=f"picked{s}", align_bytes=64) for s, w in enumerate(PICK_WIDTHS)]
+        picked = [keep.tile([P, PACK, w], F32, name=f"picked{s}", align_bytes=256) for s, w in enumerate(PICK_WIDTHS)]
         pick_starts = [sum(PICK_WIDTHS[:s]) for s in range(len(PICK_WIDTHS))]
 
         def place(j0):
             s = max(v for v in range(len(pick_starts)) if pick_starts[v] <= j0)
             return s, j0 - pick_starts[s]
 
-        x_codes = keep.tile([P, J], U32, name="x_codes", align_bytes=64)
-        x_scales = keep.tile([P, J], U8, name="x_scales", align_bytes=64)
-        wu_codes = [keep.tile([P, PASS], U32, name=f"wu_codes{a}", align_bytes=64) for a in range(HALVES)]
-        wu_scales = [keep.tile([P, PASS], U8, name=f"wu_scales{a}", align_bytes=64) for a in range(HALVES)]
-        wg_codes = [keep.tile([P, PASS], I32, name=f"wg_codes{a}", align_bytes=64) for a in range(HALVES)]
-        wd_codes = keep.tile([P, HALVES * N * 2], U8, name="wd_codes", align_bytes=64)
-        w_scales = keep.tile([P, PASS], U8, name="w_scales", align_bytes=64)
-        h_rounded = [keep.tile([P, HALVES * SLICE * PACK], BF16, name=f"h_rounded{s}", tag=f"h_rounded{s}", align_bytes=64) for s in range(SLICES)]
+        x_codes = keep.tile([P, J], U32, name="x_codes", align_bytes=256)
+        x_scales = keep.tile([P, J], U8, name="x_scales", align_bytes=256)
+        wu_codes = [keep.tile([P, PASS], U32, name=f"wu_codes{a}", align_bytes=256) for a in range(HALVES)]
+        wu_scales = [keep.tile([P, PASS], U8, name=f"wu_scales{a}", align_bytes=256) for a in range(HALVES)]
+        wg_codes = [keep.tile([P, PASS], I32, name=f"wg_codes{a}", align_bytes=256) for a in range(HALVES)]
+        wd_codes = keep.tile([P, HALVES * N * 2], U8, name="wd_codes", align_bytes=256)
+        w_scales = keep.tile([P, PASS], U8, name="w_scales", align_bytes=256)
+        h_rounded = [keep.tile([P, HALVES * SLICE * PACK], BF16, name=f"h_rounded{s}", tag=f"h_rounded{s}", align_bytes=256) for s in range(SLICES)]
         h_codes = {}
-        h_scales = [keep.tile([P, HALVES * SLICE], U8, name=f"h_scales{s}", align_bytes=64) for s in range(SLICES)]
+        h_scales = [keep.tile([P, HALVES * SLICE], U8, name=f"h_scales{s}", align_bytes=256) for s in range(SLICES)]
 
         def h_place(a, c):
             s, half = divmod(c, 2)
             return s, a * SLICE + half * CHUNK
-        out_codes = keep.tile([P, J], U32, name="out_codes", align_bytes=64)
-        out_scales = keep.tile([P, J], U8, name="out_scales", align_bytes=64)
+        out_codes = keep.tile([P, J], U32, name="out_codes", align_bytes=256)
+        out_scales = keep.tile([P, J], U8, name="out_scales", align_bytes=256)
 
         def gather(i, j0, width):
             s, at = place(j0)
@@ -133,7 +133,7 @@ def tile_list_relu_resP_kernel(tc, xT, wgt, wg_words, wg_scales, wu, wd_words, w
 
         def round_x(j0, width):
             s, at = place(j0)
-            rounded = keep.tile([P, width * PACK], BF16, name="x_rounded", tag=X_ROUNDED_IN[j0], align_bytes=64)[:]
+            rounded = keep.tile([P, width * PACK], BF16, name="x_rounded", tag=X_ROUNDED_IN[j0], align_bytes=256)[:]
             interleave(rounded, picked[s][:, :, at : at + width], nc.vector.tensor_copy if j0 == SLICE else nc.scalar.copy)
             x_rounded[j0] = rounded
 
@@ -144,7 +144,7 @@ def tile_list_relu_resP_kernel(tc, xT, wgt, wg_words, wg_scales, wu, wd_words, w
             nc.vector.quantize_mx(x_codes[:, cols].bitcast(FP8X4), x_scales[:, cols], x_rounded[j0])
 
         def quantise_wu(a):
-            rounded = keep.tile([P, PASS * PACK], BF16, name="wu_rounded", tag=f"wu_rounded{a}", align_bytes=64)
+            rounded = keep.tile([P, PASS * PACK], BF16, name="wu_rounded", tag=f"wu_rounded{a}", align_bytes=256)
             for u in range(2):
                 nc.scalar.activation(
                     rounded[:].rearrange("p (t m i) -> p m i t", t=PACK, i=PACK)[:, u * (P // 2) : (u + 1) * (P // 2)],
@@ -222,7 +222,7 @@ def tile_list_relu_resP_kernel(tc, xT, wgt, wg_words, wg_scales, wu, wd_words, w
         def quantise_h(s, at, width):
             cols = slice(at, at + width)
             if s not in h_codes:
-                h_codes[s] = keep.tile([P, HALVES * SLICE], U32, name="h_codes", tag=H_CODES_IN[s], align_bytes=64)
+                h_codes[s] = keep.tile([P, HALVES * SLICE], U32, name="h_codes", tag=H_CODES_IN[s], align_bytes=256)
             nc.vector.quantize_mx(h_codes[s][:, cols].bitcast(FP8X4), h_scales[s][:, cols], h_rounded[s][:, at * PACK : (at + width) * PACK])
 
         starts = [sum(OUT_WIDTHS[:u]) for u in range(len(OUT_WIDTHS))]
@@ -260,7 +260,7 @@ def tile_list_relu_resP_kernel(tc, xT, wgt, wg_words, wg_scales, wu, wd_words, w
 
         def add_staged(c):
             h, r0 = divmod(c * CHUNK, SLICE)
-            result = keep.tile([P, PACK, CHUNK], F32, name="result_late", tag=f"h_rounded{h + 1}", align_bytes=64)
+            result = keep.tile([P, PACK, CHUNK], F32, name="result_late", tag=f"h_rounded{h + 1}", align_bytes=256)
             nc.gpsimd.tensor_tensor(result[:], staged[c][:], res_tiles[h][:, :, r0 : r0 + CHUNK], ADD)
             finish_chunk(c, result)
 
@@ -269,7 +269,7 @@ def tile_list_relu_resP_kernel(tc, xT, wgt, wg_words, wg_scales, wu, wd_words, w
             at = c * CHUNK - starts[u]
             h, r0 = divmod(c * CHUNK, SLICE)
             if c in GPSIMD_CHUNKS:
-                staged[c] = keep.tile([P, PACK, CHUNK], F32, name=f"y_staged{c}", tag=f"y_staged{c}", align_bytes=64)
+                staged[c] = keep.tile([P, PACK, CHUNK], F32, name=f"y_staged{c}", tag=f"y_staged{c}", align_bytes=256)
                 nc.scalar.copy(staged[c][:], y[:])
             elif u < SPLIT_SLICES:
                 result = keep.tile([P, PACK, CHUNK], F32, name=f"result_odd{c}")
@@ -280,7 +280,7 @@ def tile_list_relu_resP_kernel(tc, xT, wgt, wg_words, wg_scales, wu, wd_words, w
                 if at + CHUNK == OUT_WIDTHS[u]:
                     round_out(u)
 
-        out_rounded = [keep.tile([P, w * PACK], BF16, name=f"out_rounded{u}", tag=f"out_rounded{u}", align_bytes=64) for u, w in enumerate(OUT_WIDTHS)]
+        out_rounded = [keep.tile([P, w * PACK], BF16, name=f"out_rounded{u}", tag=f"out_rounded{u}", align_bytes=256) for u, w in enumerate(OUT_WIDTHS)]
 
         def round_out(u):
             cols = slice(starts[u], starts[u] + OUT_WIDTHS[u])
@@ -291,7 +291,7 @@ def tile_list_relu_resP_kernel(tc, xT, wgt, wg_words, wg_scales, wu, wd_words, w
             cols = slice(starts[u], starts[u] + OUT_WIDTHS[u])
             end = cols.stop
             if u == 0:
-                first_codes = keep.tile([P, SLICE], U32, name="first_codes", tag="res1", align_bytes=64)
+                first_codes = keep.tile([P, SLICE], U32, name="first_codes", tag="res1", align_bytes=256)
                 nc.vector.quantize_mx(first_codes[:].bitcast(FP8X4), out_scales[:, cols], out_rounded[u][:])
                 nc.sync.dma_start(out_words[:, cols], first_codes[:].bitcast(I32))
                 return
@@ -357,7 +357,7 @@ def tile_list_relu_resP_kernel(tc, xT, wgt, wg_words, wg_scales, wu, wd_words, w
         quantise_out(0)
         quantise_h(last, SLICE + CHUNK, CHUNK)
         sums.append(down(CHUNKS - 1))
-        results[3] = keep.tile([P, PACK, CHUNK], F32, name="result3", tag=f"h_rounded{last}", align_bytes=64)
+        results[3] = keep.tile([P, PACK, CHUNK], F32, name="result3", tag=f"h_rounded{last}", align_bytes=256)
         add_res(CHUNKS - 2, sums[0])
         quantise_out(last - 2)
         add_res(CHUNKS - 1, sums[1])

@@ -47,23 +47,23 @@ def tile_list_relu_resP_kernel(tc, xT, wgt, wg_words, wg_scales, wu, wd_words, w
 
         offsets = keep.tile([P, J // 16], U16, name="offsets")
 
-        weights = keep.tile([P, J], F32, name="weights")
-        x_planes = [keep.tile([P, T], F32, name=f"x_plane{i}") for i in range(PACK)]
+        weights = keep.tile([P, J], F32, name="weights", align_bytes=256)
+        x_planes = [keep.tile([P, T], F32, name=f"x_plane{i}", align_bytes=256) for i in range(PACK)]
         x_rows = xT.rearrange("(p i) t -> i p t", i=PACK)
         wu_raw = [keep.tile([P, PACK, WU_PIECE], F32, name=f"wu_raw{u}", tag=f"wu_raw{u}", align_bytes=256) for u in range(R // WU_PIECE)]
         wu_rows = wu.rearrange("(p i) r -> p i r", i=PACK)
-        wg_raw = [keep.tile([P, PASS], I32, name=f"wg_raw{a}") for a in range(HALVES)]
+        wg_raw = [keep.tile([P, PASS], I32, name=f"wg_raw{a}", align_bytes=256) for a in range(HALVES)]
         wg_rows = wg_words[0].rearrange("p r i -> p (r i)").bitcast(I32)
-        wd_raw = keep.tile([P, HALVES * N * 2], U8, name="wd_raw")
-        scales_raw = keep.tile([P, PASS], U8, name="scales_raw")
+        wd_raw = keep.tile([P, HALVES * N * 2], U8, name="wd_raw", align_bytes=256)
+        scales_raw = keep.tile([P, PASS], U8, name="scales_raw", align_bytes=256)
         wd_late_scales = keep.tile([P, PASS], U8, name="wd_late_scales", align_bytes=256)
         res_tiles = [keep.tile([P, PACK, SLICE], F32, name=f"res{s}", tag=f"res{s}", align_bytes=256) for s in range(SLICES)]
         res_rows = res.rearrange("(p t) j -> p t j", t=PACK)
         out_rows = out_0.rearrange("(p t) j -> p t j", t=PACK)
         out_words = out_1[0].rearrange("p j i -> p (j i)").bitcast(I32)
 
-        head_rows = keep.tile([P, P], F32, name="head_rows")
-        identity = keep.tile([P, P], F32, name="identity")
+        head_rows = keep.tile([P, P], F32, name="head_rows", align_bytes=256)
+        identity = keep.tile([P, P], F32, name="identity", align_bytes=256)
         nc.sync.dma_start(head_rows[0:64, :], wgt.rearrange("(g v) (u e) -> v g u e", v=16, e=P)[0])
         nc.vector.memset(head_rows[64:P, :], 0.0)
         nc.vector.memset(scales_raw[:].bitcast(I32), 0)
@@ -194,7 +194,7 @@ def tile_list_relu_resP_kernel(tc, xT, wgt, wg_words, wg_scales, wu, wd_words, w
 
             if c0 > 1:
                 up_sums()
-            opened = ring.tile([P, CHUNK // 2, PACK, 2], F32, name="opened", bufs=4)
+            opened = ring.tile([P, CHUNK // 2, PACK, 2], F32, name="opened", align_bytes=256, bufs=4)
             per_bank = PACK // count
             for bank in range(count):
                 gate = psum.tile([P, per_bank, width], F32, name="gate", tag="gate", bufs=3)
@@ -226,7 +226,7 @@ def tile_list_relu_resP_kernel(tc, xT, wgt, wg_words, wg_scales, wu, wd_words, w
             nc.vector.quantize_mx(h_codes[s][:, cols].bitcast(FP8X4), h_scales[s][:, cols], h_rounded[s][:, at * PACK : (at + width) * PACK])
 
         starts = [sum(OUT_WIDTHS[:u]) for u in range(len(OUT_WIDTHS))]
-        results = {u: keep.tile([P, PACK, w], F32, name=f"result{u}") for u, w in enumerate(OUT_WIDTHS) if u in (2, 4)}
+        results = {u: keep.tile([P, PACK, w], F32, name=f"result{u}", align_bytes=256) for u, w in enumerate(OUT_WIDTHS) if u in (2, 4)}
 
         def down(c):
             late = c >= CHUNKS - 2
@@ -272,7 +272,7 @@ def tile_list_relu_resP_kernel(tc, xT, wgt, wg_words, wg_scales, wu, wd_words, w
                 staged[c] = keep.tile([P, PACK, CHUNK], F32, name=f"y_staged{c}", tag=f"y_staged{c}", align_bytes=256)
                 nc.scalar.copy(staged[c][:], y[:])
             elif u < SPLIT_SLICES:
-                result = keep.tile([P, PACK, CHUNK], F32, name=f"result_odd{c}")
+                result = keep.tile([P, PACK, CHUNK], F32, name=f"result_odd{c}", align_bytes=256)
                 nc.vector.tensor_tensor(result[:], y[:], res_tiles[h][:, :, r0 : r0 + CHUNK], ADD)
                 finish_chunk(c, result)
             else:
@@ -303,7 +303,7 @@ def tile_list_relu_resP_kernel(tc, xT, wgt, wg_words, wg_scales, wu, wd_words, w
         nc.tensor.transpose(turned[:], head_rows[:], identity[:])
         u0 = 0
         for part, count in enumerate(SPREAD_PARTS):
-            spread = keep.tile([P, count, 8, 16], F32, name=f"spread{part}")
+            spread = keep.tile([P, count, 8, 16], F32, name=f"spread{part}", align_bytes=256)
             nc.scalar.copy(spread[:], turned[:, 0:64].rearrange("e (g u) -> e u g", u=8)[:, u0 : u0 + count, :].unsqueeze(3).to_broadcast([P, count, 8, 16]))
             back = psum.tile([P, count, P], F32, name="back", tag="gate", bufs=3)
             for u in range(count):

@@ -25,103 +25,110 @@ PASS = P * PACK
 HALVES = R // PASS
 CHUNK = 128
 CHUNKS = J // CHUNK
-SLICE = 256
+SLICE = 2 * CHUNK
 SLICES = J // SLICE
-WG_ROW = 8
+HEADS = 8
+GROUP = P // HEADS
+ALIGN = 256
+WG_ROW = 4
 WU_PIECE = PASS // 2
-OUT_WIDTHS = (256, 256, 256, 128, 128)
-SPLIT_SLICES = 2
-H_CODES_IN = ("h_codes0", "wu_raw3", "h_codes2", "y_staged2")
-PICK_WIDTHS = (1024,)
+OUT_WIDTHS = (SLICE, SLICE, SLICE, CHUNK, CHUNK)
+CHUNKWISE_SLICES = 2
 GPSIMD_CHUNKS = (0, 2)
 SPREAD_PARTS = (2, 3, 3)
-X_ROUNDED_IN = {0: "x_first", 128: "wu_raw1", 256: "wu_rounded0", 512: "wu_raw3", 768: "wu_raw3"}
+UP_BANKS, GATE_BANKS, Y_BANKS = 3, 3, 2
+RELU_BUFFERS = GATE_BANKS + 1
+
+X_ROUNDED_IN = {0: "x_first", CHUNK: "wu_raw1", SLICE: "wu_rounded0", 2 * SLICE: "wu_raw3", 3 * SLICE: "wu_raw3"}
+H_CODES_IN = ("h_codes0", "wu_raw3", "h_codes2", "y_staged2")
+W_SCALES_IN = ("w_scales0", "wg_raw1")
 
 
 def tile_list_relu_resP_kernel(tc, xT, wgt, wg_words, wg_scales, wu, wd_words, wd_scales, res, offs, out_0, out_1, out_2):
     nc = tc.nc
     with ExitStack() as ctx:
         keep = ctx.enter_context(tc.tile_pool(name="keep", bufs=1))
-        ring = ctx.enter_context(tc.tile_pool(name="ring", bufs=3))
+        ring = ctx.enter_context(tc.tile_pool(name="ring", bufs=RELU_BUFFERS))
         psum = ctx.enter_context(tc.psum_pool(name="psum", bufs=1))
 
-        offsets = keep.tile([P, J // 16], U16, name="offsets")
+        def tile(shape, dtype, tag):
+            return keep.tile(shape, dtype, name=tag, tag=tag, align_bytes=ALIGN)
 
-        weights = keep.tile([P, J], F32, name="weights", align_bytes=256)
-        x_planes = [keep.tile([P, T], F32, name=f"x_plane{i}", align_bytes=256) for i in range(PACK)]
+        offsets = keep.tile([P, J // GROUP], U16, name="offsets")
+
+        weights = tile([P, J], F32, "weights")
+        x_planes = [tile([P, T], F32, f"x_plane{i}") for i in range(PACK)]
         x_rows = xT.rearrange("(p i) t -> i p t", i=PACK)
-        wu_raw = [keep.tile([P, PACK, WU_PIECE], F32, name=f"wu_raw{u}", tag=f"wu_raw{u}", align_bytes=256) for u in range(R // WU_PIECE)]
+        wu_raw = [tile([P, PACK, WU_PIECE], F32, f"wu_raw{u}") for u in range(R // WU_PIECE)]
         wu_rows = wu.rearrange("(p i) r -> p i r", i=PACK)
-        wg_raw = [keep.tile([P, PASS], I32, name=f"wg_raw{a}", align_bytes=256) for a in range(HALVES)]
+        wg_raw = [tile([P, PASS], I32, f"wg_raw{a}") for a in range(HALVES)]
         wg_rows = wg_words[0].rearrange("p r i -> p (r i)").bitcast(I32)
-        wd_raw = keep.tile([P, HALVES * N * 2], U8, name="wd_raw", align_bytes=256)
-        scales_raw = keep.tile([P, PASS], U8, name="scales_raw", align_bytes=256)
-        wd_late_scales = keep.tile([P, PASS], U8, name="wd_late_scales", align_bytes=256)
-        res_tiles = [keep.tile([P, PACK, SLICE], F32, name=f"res{s}", tag=f"res{s}", align_bytes=256) for s in range(SLICES)]
+        wd_raw = tile([P, HALVES * N * 2], U8, "wd_raw")
+        scales_raw = tile([P, R], U8, "scales_raw")
+        res_tiles = [tile([P, PACK, SLICE], F32, f"res{s}") for s in range(SLICES)]
         res_rows = res.rearrange("(p t) j -> p t j", t=PACK)
         out_rows = out_0.rearrange("(p t) j -> p t j", t=PACK)
         out_words = out_1[0].rearrange("p j i -> p (j i)").bitcast(I32)
 
-        head_rows = keep.tile([P, P], F32, name="head_rows", align_bytes=256)
-        identity = keep.tile([P, P], F32, name="identity", align_bytes=256)
-        nc.sync.dma_start(head_rows[0:64, :], wgt.rearrange("(g v) (u e) -> v g u e", v=16, e=P)[0])
-        nc.vector.memset(head_rows[64:P, :], 0.0)
+        head_rows = tile([P, P], F32, "head_rows")
+        identity = tile([P, P], F32, "identity")
+        live = HEADS * CHUNKS
+        nc.sync.dma_start(head_rows[0:live, :], wgt.rearrange("(g v) (u e) -> v g u e", v=GROUP, e=P)[0])
+        nc.vector.memset(head_rows[live:P, :], 0.0)
         nc.vector.memset(scales_raw[:].bitcast(I32), 0)
         make_identity(nc, identity[:])
-        nc.gpsimd.memset(wd_late_scales[:].bitcast(I32), 0)
+
+        def load_wu(u):
+            nc.sync.dma_start(wu_raw[u][:], wu_rows[:, :, u * WU_PIECE : (u + 1) * WU_PIECE])
+
+        def load_res(s):
+            nc.sync.dma_start(res_tiles[s][:], res_rows[:, :, s * SLICE : (s + 1) * SLICE])
 
         nc.sync.dma_start(x_planes[0][:], x_rows[0])
         nc.sync.dma_start(offsets[:], offs)
         nc.sync.dma_start(x_planes[1][:], x_rows[1])
         for q in range(4):
             nc.sync.dma_start(
-                scales_raw[32 * q + WG_ROW : 32 * q + WG_ROW + 8, :].bitcast(I32),
-                wg_scales[0, 4 * q : 4 * q + 4, :].bitcast(I32).rearrange("r (a n) -> a r n", a=HALVES),
+                scales_raw[32 * q + WG_ROW : 32 * q + WG_ROW + 4, :].bitcast(I32),
+                wg_scales[0, 4 * q : 4 * q + 4, :].bitcast(I32),
             )
         nc.sync.dma_start(x_planes[2][:], x_rows[2])
         nc.sync.dma_start(x_planes[3][:], x_rows[3])
         for q in range(4):
             nc.sync.dma_start(
-                scales_raw[32 * q : 32 * q + 8, :].bitcast(I32),
-                wd_scales[:, 4 * q : 4 * q + 4, :].bitcast(I32),
+                scales_raw[32 * q : 32 * q + 4, :].bitcast(I32).rearrange("r (a n) -> r a n", a=HALVES),
+                wd_scales[:, 4 * q : 4 * q + 4, :].bitcast(I32).rearrange("a r n -> r a n"),
             )
-        for u in range(2):
-            nc.sync.dma_start(wu_raw[u][:], wu_rows[:, :, u * WU_PIECE : (u + 1) * WU_PIECE])
-        nc.sync.dma_start(wg_raw[0][:], wg_rows[:, 0:PASS])
-        nc.sync.dma_start(wg_raw[1][:], wg_rows[:, PASS:R])
-        for u in range(2, 4):
-            nc.sync.dma_start(wu_raw[u][:], wu_rows[:, :, u * WU_PIECE : (u + 1) * WU_PIECE])
+        load_wu(0)
+        load_wu(1)
+        for a in range(HALVES):
+            nc.sync.dma_start(wg_raw[a][:], wg_rows[:, a * PASS : (a + 1) * PASS])
+        load_wu(2)
+        load_wu(3)
         nc.sync.dma_start(wd_raw[:].bitcast(I32).rearrange("p (a w) -> p a w", a=HALVES), wd_words.bitcast(I32).rearrange("a p w -> p a w"))
-        nc.sync.dma_start(res_tiles[0][:], res_rows[:, :, 0:SLICE])
+        load_res(0)
 
-        picked = [keep.tile([P, PACK, w], F32, name=f"picked{s}", align_bytes=256) for s, w in enumerate(PICK_WIDTHS)]
-        pick_starts = [sum(PICK_WIDTHS[:s]) for s in range(len(PICK_WIDTHS))]
-
-        def place(j0):
-            s = max(v for v in range(len(pick_starts)) if pick_starts[v] <= j0)
-            return s, j0 - pick_starts[s]
-
-        x_codes = keep.tile([P, J], U32, name="x_codes", align_bytes=256)
-        x_scales = keep.tile([P, J], U8, name="x_scales", align_bytes=256)
-        wu_codes = [keep.tile([P, PASS], U32, name=f"wu_codes{a}", align_bytes=256) for a in range(HALVES)]
-        wu_scales = [keep.tile([P, PASS], U8, name=f"wu_scales{a}", align_bytes=256) for a in range(HALVES)]
-        wg_codes = [keep.tile([P, PASS], I32, name=f"wg_codes{a}", align_bytes=256) for a in range(HALVES)]
-        wd_codes = keep.tile([P, HALVES * N * 2], U8, name="wd_codes", align_bytes=256)
-        w_scales = keep.tile([P, PASS], U8, name="w_scales", align_bytes=256)
-        h_rounded = [keep.tile([P, HALVES * SLICE * PACK], BF16, name=f"h_rounded{s}", tag=f"h_rounded{s}", align_bytes=256) for s in range(SLICES)]
+        picked = tile([P, PACK, J], F32, "picked")
+        x_codes = tile([P, J], U32, "x_codes")
+        x_scales = tile([P, J], U8, "x_scales")
+        wu_codes = [tile([P, PASS], U32, f"wu_codes{a}") for a in range(HALVES)]
+        wu_scales = [tile([P, PASS], U8, f"wu_scales{a}") for a in range(HALVES)]
+        wg_codes = [tile([P, PASS], I32, f"wg_codes{a}") for a in range(HALVES)]
+        wd_codes = tile([P, HALVES * N * 2], U8, "wd_codes")
+        w_scales = {}
+        h_rounded = [tile([P, HALVES * SLICE * PACK], BF16, f"h_rounded{s}") for s in range(SLICES)]
         h_codes = {}
-        h_scales = [keep.tile([P, HALVES * SLICE], U8, name=f"h_scales{s}", align_bytes=256) for s in range(SLICES)]
+        h_scales = [tile([P, HALVES * SLICE], U8, f"h_scales{s}") for s in range(SLICES)]
+        out_codes = tile([P, J], U32, "out_codes")
+        out_scales = tile([P, J], U8, "out_scales")
 
         def h_place(a, c):
             s, half = divmod(c, 2)
             return s, a * SLICE + half * CHUNK
-        out_codes = keep.tile([P, J], U32, name="out_codes", align_bytes=256)
-        out_scales = keep.tile([P, J], U8, name="out_scales", align_bytes=256)
 
         def gather(i, j0, width):
-            s, at = place(j0)
-            entries = offsets[:, j0 // 16 : (j0 + width) // 16]
-            nc.vector.tensor_tensor(picked[s][:, i, at : at + width], x_planes[i][:].indirect(entries), weights[:, j0 : j0 + width], MULT)
+            entries = offsets[:, j0 // GROUP : (j0 + width) // GROUP]
+            nc.vector.tensor_tensor(picked[:, i, j0 : j0 + width], x_planes[i][:].indirect(entries), weights[:, j0 : j0 + width], MULT)
 
         def interleave(rounded, planes, copy=nc.scalar.copy):
             copy(
@@ -129,25 +136,18 @@ def tile_list_relu_resP_kernel(tc, xT, wgt, wg_words, wg_scales, wu, wd_words, w
                 planes.rearrange("p t (c e) -> p c t e", e=4),
             )
 
-        x_rounded = {}
-
-        def round_x(j0, width):
-            s, at = place(j0)
-            rounded = keep.tile([P, width * PACK], BF16, name="x_rounded", tag=X_ROUNDED_IN[j0], align_bytes=256)[:]
-            interleave(rounded, picked[s][:, :, at : at + width], nc.vector.tensor_copy if j0 == SLICE else nc.scalar.copy)
-            x_rounded[j0] = rounded
-
         def quantise_x(j0, width):
-            if j0 not in x_rounded:
-                round_x(j0, width)
+            rounded = tile([P, width * PACK], BF16, X_ROUNDED_IN[j0])
             cols = slice(j0, j0 + width)
-            nc.vector.quantize_mx(x_codes[:, cols].bitcast(FP8X4), x_scales[:, cols], x_rounded[j0])
+            interleave(rounded[:], picked[:, :, cols], nc.vector.tensor_copy if j0 == SLICE else nc.scalar.copy)
+            nc.vector.quantize_mx(x_codes[:, cols].bitcast(FP8X4), x_scales[:, cols], rounded[:])
 
         def quantise_wu(a):
-            rounded = keep.tile([P, PASS * PACK], BF16, name="wu_rounded", tag=f"wu_rounded{a}", align_bytes=256)
-            for u in range(2):
+            rounded = tile([P, PASS * PACK], BF16, f"wu_rounded{a}")
+            places = WU_PIECE // PACK
+            for u in range(PASS // WU_PIECE):
                 nc.scalar.activation(
-                    rounded[:].rearrange("p (t m i) -> p m i t", t=PACK, i=PACK)[:, u * (P // 2) : (u + 1) * (P // 2)],
+                    rounded[:].rearrange("p (t m i) -> p m i t", t=PACK, i=PACK)[:, u * places : (u + 1) * places],
                     wu_raw[2 * a + u][:].rearrange("p i (m t) -> p m i t", t=PACK),
                     COPY,
                 )
@@ -159,15 +159,12 @@ def tile_list_relu_resP_kernel(tc, xT, wgt, wg_words, wg_scales, wu, wd_words, w
                 wg_raw[a][:].rearrange("p (c e t) -> p c t e", t=PACK, e=4),
             )
 
-        def deal_scales():
+        def deal_scales(a):
+            w_scales[a] = tile([P, PASS], U8, W_SCALES_IN[a])
             nc.vector.tensor_copy(
-                w_scales[:].rearrange("p (t m) -> p t m", t=PACK),
-                scales_raw[:].rearrange("p (m t) -> p t m", t=PACK),
+                w_scales[a][:].rearrange("p (t m) -> p t m", t=PACK),
+                scales_raw[:, a * PASS : (a + 1) * PASS].rearrange("p (m t) -> p t m", t=PACK),
             )
-
-        def carry_scales():
-            for q in range(4):
-                nc.sync.dma_start(wd_late_scales[32 * q : 32 * q + 4, :].bitcast(I32), w_scales[32 * q + 4 : 32 * q + 8, :].bitcast(I32))
 
         def deal_wd():
             nc.vector.tensor_copy(
@@ -175,62 +172,58 @@ def tile_list_relu_resP_kernel(tc, xT, wgt, wg_words, wg_scales, wu, wd_words, w
                 wd_raw[:].bitcast(U16).rearrange("p (a m t) -> p a t m", a=HALVES, t=PACK),
             )
 
-        def product(out, codes, scales, cols):
-            nc.tensor.matmul_mx(out, lhsT=codes.bitcast(FP8X4), lhsT_scale=scales, rhs=x_codes[:, cols].bitcast(FP8X4), rhs_scale=x_scales[:, cols], start=True, stop=True)
-
-        ready = {}
-
-        def sums_of(a, c0, count):
-            width = count * CHUNK
-            ups = []
-
-            def up_sums():
-                for c in range(c0, c0 + count):
-                    final = (a, c) == (HALVES - 1, CHUNKS - 1)
-                    up = psum.tile([P, PACK, CHUNK], F32, name="up", tag="y" if final else "up", bufs=2 if final else 3)
-                    for t in range(PACK):
-                        product(up[:, t, :], wu_codes[a][:, t * P : (t + 1) * P], wu_scales[a][:, t * P : (t + 1) * P], slice(c * CHUNK, (c + 1) * CHUNK))
-                    ups.append(up)
-
-            if c0 > 1:
-                up_sums()
-            opened = ring.tile([P, CHUNK // 2, PACK, 2], F32, name="opened", align_bytes=256, bufs=4)
-            per_bank = PACK // count
-            for bank in range(count):
-                gate = psum.tile([P, per_bank, width], F32, name="gate", tag="gate", bufs=3)
-                for v in range(per_bank):
-                    t = bank * per_bank + v
-                    product(gate[:, v, :], wg_codes[a][:, t * P : (t + 1) * P], w_scales[WG_ROW + 4 * a : P, t * P : (t + 1) * P], slice(c0 * CHUNK, c0 * CHUNK + width))
-                nc.scalar.activation(opened[:, 0 : width // 2, bank * per_bank : (bank + 1) * per_bank, :], gate[:].rearrange("p t (c e) -> p c t e", e=2), RELU)
-            if c0 <= 1:
-                up_sums()
-            for v in range(count):
-                ready[a, c0 + v] = (ups[v], opened[:, v * CHUNK // 2 : (v + 1) * CHUNK // 2])
+        def sums_with_x(bank, codes, scales, c):
+            cols = slice(c * CHUNK, (c + 1) * CHUNK)
+            for t in range(PACK):
+                nc.tensor.matmul_mx(
+                    bank[:, t, :],
+                    lhsT=codes[:, t * P : (t + 1) * P].bitcast(FP8X4),
+                    lhsT_scale=scales[:, t * P : (t + 1) * P],
+                    rhs=x_codes[:, cols].bitcast(FP8X4),
+                    rhs_scale=x_scales[:, cols],
+                    start=True,
+                    stop=True,
+                )
 
         def hidden(a, c):
-            if (a, c) not in ready:
-                sums_of(a, c, 1)
-            up, opened = ready[a, c]
+            def up_sums():
+                if (a, c) == (HALVES - 1, CHUNKS - 1):
+                    bank = psum.tile([P, PACK, CHUNK], F32, name="y", tag="y", bufs=Y_BANKS)
+                else:
+                    bank = psum.tile([P, PACK, CHUNK], F32, name="up", tag="up", bufs=UP_BANKS)
+                sums_with_x(bank, wu_codes[a][:], wu_scales[a][:], c)
+                return bank
+
+            up = up_sums() if c * CHUNK >= SLICE else None
+            opened = ring.tile([P, CHUNK // 2, PACK, 2], F32, name="opened", align_bytes=ALIGN)
+            gate = psum.tile([P, PACK, CHUNK], F32, name="gate", tag="gate", bufs=GATE_BANKS)
+            sums_with_x(gate, wg_codes[a][:], w_scales[a][WG_ROW:P, :], c)
+            nc.scalar.activation(opened[:], gate[:].rearrange("p t (c e) -> p c t e", e=2), RELU)
+            if up is None:
+                up = up_sums()
             s, at = h_place(a, c)
             nc.vector.tensor_tensor(
                 h_rounded[s][:, at * PACK : (at + CHUNK) * PACK].rearrange("p (c e t) -> p c t e", e=2, t=PACK),
                 up[:].rearrange("p t (c e) -> p c t e", e=2),
-                opened,
+                opened[:],
                 MULT,
             )
 
         def quantise_h(s, at, width):
             cols = slice(at, at + width)
             if s not in h_codes:
-                h_codes[s] = keep.tile([P, HALVES * SLICE], U32, name="h_codes", tag=H_CODES_IN[s], align_bytes=256)
+                h_codes[s] = tile([P, HALVES * SLICE], U32, H_CODES_IN[s])
             nc.vector.quantize_mx(h_codes[s][:, cols].bitcast(FP8X4), h_scales[s][:, cols], h_rounded[s][:, at * PACK : (at + width) * PACK])
 
         starts = [sum(OUT_WIDTHS[:u]) for u in range(len(OUT_WIDTHS))]
-        results = {u: keep.tile([P, PACK, w], F32, name=f"result{u}", align_bytes=256) for u, w in enumerate(OUT_WIDTHS) if u in (2, 4)}
+        last = SLICES - 1
+        results = {u: tile([P, PACK, OUT_WIDTHS[u]], F32, f"result{u}") for u in (last - 1, last + 1)}
 
         def down(c):
-            late = c >= CHUNKS - 2
-            y = psum.tile([P, PACK, CHUNK], F32, name="y", tag="gate" if late else "y", bufs=3 if late else 2)
+            if c >= CHUNKS - 2:
+                y = psum.tile([P, PACK, CHUNK], F32, name="gate", tag="gate", bufs=GATE_BANKS)
+            else:
+                y = psum.tile([P, PACK, CHUNK], F32, name="y", tag="y", bufs=Y_BANKS)
             for a in range(HALVES):
                 s, at = h_place(a, c)
                 cols = slice(at, at + CHUNK)
@@ -238,7 +231,7 @@ def tile_list_relu_resP_kernel(tc, xT, wgt, wg_words, wg_scales, wu, wd_words, w
                     nc.tensor.matmul_mx(
                         y[:, t, :],
                         lhsT=wd_codes[:, 2 * (a * PASS + t * P) : 2 * (a * PASS + (t + 1) * P)].bitcast(FP4X4),
-                        lhsT_scale=(w_scales, wd_late_scales)[a][:, t * P : (t + 1) * P],
+                        lhsT_scale=w_scales[a][:, t * P : (t + 1) * P],
                         rhs=h_codes[s][:, cols].bitcast(FP8X4),
                         rhs_scale=h_scales[s][:, cols],
                         start=(a == 0 and t == 0),
@@ -247,65 +240,61 @@ def tile_list_relu_resP_kernel(tc, xT, wgt, wg_words, wg_scales, wu, wd_words, w
             return y
 
         staged = {}
-
         chunk_results = {}
+        out_rounded = [tile([P, w * PACK], BF16, f"out_rounded{u}") for u, w in enumerate(OUT_WIDTHS)]
 
-        def finish_chunk(c, result):
+        def res_of(c):
+            s, half = divmod(c, 2)
+            return res_tiles[s][:, :, half * CHUNK : (half + 1) * CHUNK]
+
+        def store_chunk(c, result):
             nc.sync.dma_start(out_rows[:, :, c * CHUNK : (c + 1) * CHUNK], result[:])
             chunk_results[c] = result
 
         def round_chunk(c):
-            u, half = divmod(c, 2)
-            interleave(out_rounded[u][:, half * CHUNK * PACK : (half + 1) * CHUNK * PACK], chunk_results[c][:])
+            s, half = divmod(c, 2)
+            interleave(out_rounded[s][:, half * CHUNK * PACK : (half + 1) * CHUNK * PACK], chunk_results[c][:])
 
         def add_staged(c):
-            h, r0 = divmod(c * CHUNK, SLICE)
-            result = keep.tile([P, PACK, CHUNK], F32, name="result_late", tag=f"h_rounded{h + 1}", align_bytes=256)
-            nc.gpsimd.tensor_tensor(result[:], staged[c][:], res_tiles[h][:, :, r0 : r0 + CHUNK], ADD)
-            finish_chunk(c, result)
+            result = tile([P, PACK, CHUNK], F32, f"h_rounded{c // 2 + 1}")
+            nc.gpsimd.tensor_tensor(result[:], staged[c][:], res_of(c), ADD)
+            store_chunk(c, result)
 
         def add_res(c, y):
             u = max(v for v in range(len(starts)) if starts[v] <= c * CHUNK)
             at = c * CHUNK - starts[u]
-            h, r0 = divmod(c * CHUNK, SLICE)
             if c in GPSIMD_CHUNKS:
-                staged[c] = keep.tile([P, PACK, CHUNK], F32, name=f"y_staged{c}", tag=f"y_staged{c}", align_bytes=256)
+                staged[c] = tile([P, PACK, CHUNK], F32, f"y_staged{c}")
                 nc.scalar.copy(staged[c][:], y[:])
-            elif u < SPLIT_SLICES:
-                result = keep.tile([P, PACK, CHUNK], F32, name=f"result_odd{c}", align_bytes=256)
-                nc.vector.tensor_tensor(result[:], y[:], res_tiles[h][:, :, r0 : r0 + CHUNK], ADD)
-                finish_chunk(c, result)
+            elif u < CHUNKWISE_SLICES:
+                result = tile([P, PACK, CHUNK], F32, f"result_odd{c}")
+                nc.vector.tensor_tensor(result[:], y[:], res_of(c), ADD)
+                store_chunk(c, result)
             else:
-                nc.vector.tensor_tensor(results[u][:, :, at : at + CHUNK], y[:], res_tiles[h][:, :, r0 : r0 + CHUNK], ADD)
+                nc.vector.tensor_tensor(results[u][:, :, at : at + CHUNK], y[:], res_of(c), ADD)
                 if at + CHUNK == OUT_WIDTHS[u]:
-                    round_out(u)
-
-        out_rounded = [keep.tile([P, w * PACK], BF16, name=f"out_rounded{u}", tag=f"out_rounded{u}", align_bytes=256) for u, w in enumerate(OUT_WIDTHS)]
-
-        def round_out(u):
-            cols = slice(starts[u], starts[u] + OUT_WIDTHS[u])
-            nc.sync.dma_start(out_rows[:, :, cols], results[u][:])
-            interleave(out_rounded[u][:], results[u][:], nc.vector.tensor_copy if u == len(OUT_WIDTHS) - 1 else nc.scalar.copy)
+                    nc.sync.dma_start(out_rows[:, :, starts[u] : starts[u] + OUT_WIDTHS[u]], results[u][:])
+                    interleave(out_rounded[u][:], results[u][:], nc.vector.tensor_copy if c == CHUNKS - 1 else nc.scalar.copy)
 
         def quantise_out(u):
             cols = slice(starts[u], starts[u] + OUT_WIDTHS[u])
-            end = cols.stop
             if u == 0:
-                first_codes = keep.tile([P, SLICE], U32, name="first_codes", tag="res1", align_bytes=256)
+                first_codes = tile([P, SLICE], U32, "res1")
                 nc.vector.quantize_mx(first_codes[:].bitcast(FP8X4), out_scales[:, cols], out_rounded[u][:])
                 nc.sync.dma_start(out_words[:, cols], first_codes[:].bitcast(I32))
                 return
             nc.vector.quantize_mx(out_codes[:, cols].bitcast(FP8X4), out_scales[:, cols], out_rounded[u][:])
-            if end % SLICE == 0:
-                nc.sync.dma_start(out_words[:, end - SLICE : end], out_codes[:, end - SLICE : end].bitcast(I32))
+            if cols.stop % SLICE == 0:
+                whole = slice(cols.stop - SLICE, cols.stop)
+                nc.sync.dma_start(out_words[:, whole], out_codes[:, whole].bitcast(I32))
 
-        turned = psum.tile([P, P], F32, name="turned", tag="y", bufs=2)
+        turned = psum.tile([P, P], F32, name="turned", tag="y", bufs=Y_BANKS)
         nc.tensor.transpose(turned[:], head_rows[:], identity[:])
         u0 = 0
         for part, count in enumerate(SPREAD_PARTS):
-            spread = keep.tile([P, count, 8, 16], F32, name=f"spread{part}", align_bytes=256)
-            nc.scalar.copy(spread[:], turned[:, 0:64].rearrange("e (g u) -> e u g", u=8)[:, u0 : u0 + count, :].unsqueeze(3).to_broadcast([P, count, 8, 16]))
-            back = psum.tile([P, count, P], F32, name="back", tag="gate", bufs=3)
+            spread = tile([P, count, HEADS, GROUP], F32, f"spread{part}")
+            nc.scalar.copy(spread[:], turned[:, 0:live].rearrange("e (g u) -> e u g", u=CHUNKS)[:, u0 : u0 + count, :].unsqueeze(3).to_broadcast([P, count, HEADS, GROUP]))
+            back = psum.tile([P, count, P], F32, name="back", tag="gate", bufs=GATE_BANKS)
             for u in range(count):
                 nc.tensor.transpose(back[:, u, :], spread[:, u].rearrange("e g v -> e (g v)"), identity[:])
             (nc.vector.tensor_copy if part == 0 else nc.scalar.copy)(weights[:, u0 * P : (u0 + count) * P], back[:].rearrange("p u e -> p (u e)"))
@@ -313,21 +302,20 @@ def tile_list_relu_resP_kernel(tc, xT, wgt, wg_words, wg_scales, wu, wd_words, w
             u0 = u0 + count
         for i in range(1, PACK - 1):
             gather(i, 0, J)
-        for j0, width in ((0, CHUNK), (CHUNK, J - CHUNK)):
-            gather(PACK - 1, j0, width)
+        gather(PACK - 1, 0, CHUNK)
+        gather(PACK - 1, CHUNK, J - CHUNK)
         quantise_x(0, CHUNK)
-        deal_scales()
-        carry_scales()
+        deal_scales(0)
         for s in range(1, SLICES):
-            nc.sync.dma_start(res_tiles[s][:], res_rows[:, :, s * SLICE : (s + 1) * SLICE])
+            load_res(s)
         deal_wg(0)
         quantise_wu(0)
         deal_wg(1)
         quantise_x(CHUNK, CHUNK)
 
         hidden(0, 0)
+        deal_scales(1)
         hidden(0, 1)
-        round_x(SLICE, SLICE)
         quantise_x(SLICE, SLICE)
         deal_wd()
         quantise_wu(1)
@@ -335,7 +323,7 @@ def tile_list_relu_resP_kernel(tc, xT, wgt, wg_words, wg_scales, wu, wd_words, w
         hidden(1, 1)
         for s in range(1, SLICES):
             c = 2 * s
-            if s + 1 < SLICES:
+            if s < last:
                 quantise_x((s + 1) * SLICE, SLICE)
             hidden(0, c)
             quantise_h(s - 1, 0, HALVES * SLICE)
@@ -349,15 +337,14 @@ def tile_list_relu_resP_kernel(tc, xT, wgt, wg_words, wg_scales, wu, wd_words, w
             if s > 1:
                 round_chunk(c - 3)
                 round_chunk(c - 4)
-            if s + 1 == SLICES:
+            if s == last:
                 quantise_h(s, 0, SLICE + CHUNK)
             hidden(1, c + 1)
-        last = SLICES - 1
         sums = [down(CHUNKS - 2)]
         quantise_out(0)
         quantise_h(last, SLICE + CHUNK, CHUNK)
         sums.append(down(CHUNKS - 1))
-        results[3] = keep.tile([P, PACK, CHUNK], F32, name="result3", tag=f"h_rounded{last}", align_bytes=256)
+        results[last] = tile([P, PACK, CHUNK], F32, f"h_rounded{last}")
         add_res(CHUNKS - 2, sums[0])
         quantise_out(last - 2)
         add_res(CHUNKS - 1, sums[1])

from contextlib import ExitStack

import concourse.mybir as mybir
from concourse.masks import make_identity

K, R, N, T, J = 512, 1024, 512, 2048, 1024
FLOPS = 2 * K * R * J * 2 + 2 * R * N * J

F32 = mybir.dt.float32
BF16 = mybir.dt.bfloat16
I32 = mybir.dt.int32
U32 = mybir.dt.uint32
U16 = mybir.dt.uint16
U8 = mybir.dt.uint8
FP8X4 = mybir.dt.float8_e4m3fn_x4
FP4X4 = mybir.dt.float4_e2m1fn_x4
MULT = mybir.AluOpType.mult
ADD = mybir.AluOpType.add
RELU = mybir.ActivationFunctionType.Relu
COPY = mybir.ActivationFunctionType.Copy

P = 128
PACK = 4
PASS = P * PACK
HALVES = R // PASS
CHUNK = 128
CHUNKS = J // CHUNK
SLICE = 2 * CHUNK
SLICES = J // SLICE
HEADS = 8
GROUP = P // HEADS
ALIGN = 256
WG_ROW = 4
WU_PIECE = PASS // 2
OUT_WIDTHS = (SLICE, SLICE, SLICE, CHUNK, CHUNK)
CHUNKWISE_SLICES = 2
GPSIMD_CHUNKS = (0, 2)
SPREAD_PARTS = (2, 3, 3)
UP_BANKS, GATE_BANKS, Y_BANKS = 3, 3, 2
RELU_BUFFERS = GATE_BANKS + 1

X_ROUNDED_IN = {0: "x_first", CHUNK: "wu_raw1", SLICE: "wu_rounded0", 2 * SLICE: "wu_raw3", 3 * SLICE: "wu_raw3"}
H_CODES_IN = ("h_codes0", "wu_raw3", "h_codes2", "y_staged2")
W_SCALES_IN = ("w_scales0", "wg_raw1")


def tile_list_relu_resP_kernel(tc, xT, wgt, wg_words, wg_scales, wu, wd_words, wd_scales, res, offs, out_0, out_1, out_2):
    nc = tc.nc
    with ExitStack() as ctx:
        keep = ctx.enter_context(tc.tile_pool(name="keep", bufs=1))
        ring = ctx.enter_context(tc.tile_pool(name="ring", bufs=RELU_BUFFERS))
        psum = ctx.enter_context(tc.psum_pool(name="psum", bufs=1))

        def tile(shape, dtype, tag):
            return keep.tile(shape, dtype, name=tag, tag=tag, align_bytes=ALIGN)

        offsets = keep.tile([P, J // GROUP], U16, name="offsets")

        weights = tile([P, J], F32, "weights")
        x_planes = [tile([P, T], F32, f"x_plane{i}") for i in range(PACK)]
        x_rows = xT.rearrange("(p i) t -> i p t", i=PACK)
        wu_raw = [tile([P, PACK, WU_PIECE], F32, f"wu_raw{u}") for u in range(R // WU_PIECE)]
        wu_rows = wu.rearrange("(p i) r -> p i r", i=PACK)
        wg_raw = [tile([P, PASS], I32, f"wg_raw{a}") for a in range(HALVES)]
        wg_rows = wg_words[0].rearrange("p r i -> p (r i)").bitcast(I32)
        wd_raw = tile([P, HALVES * N * 2], U8, "wd_raw")
        scales_raw = tile([P, R], U8, "scales_raw")
        res_tiles = [tile([P, PACK, SLICE], F32, f"res{s}") for s in range(SLICES)]
        res_rows = res.rearrange("(p t) j -> p t j", t=PACK)
        out_rows = out_0.rearrange("(p t) j -> p t j", t=PACK)
        out_words = out_1[0].rearrange("p j i -> p (j i)").bitcast(I32)

        head_rows = tile([P, P], F32, "head_rows")
        identity = tile([P, P], F32, "identity")
        live = HEADS * CHUNKS
        nc.sync.dma_start(head_rows[0:live, :], wgt.rearrange("(g v) (u e) -> v g u e", v=GROUP, e=P)[0])
        nc.vector.memset(head_rows[live:P, :], 0.0)
        nc.vector.memset(scales_raw[:].bitcast(I32), 0)
        make_identity(nc, identity[:])

        def load_wu(u):
            nc.sync.dma_start(wu_raw[u][:], wu_rows[:, :, u * WU_PIECE : (u + 1) * WU_PIECE])

        def load_res(s):
            nc.sync.dma_start(res_tiles[s][:], res_rows[:, :, s * SLICE : (s + 1) * SLICE])

        nc.sync.dma_start(x_planes[0][:], x_rows[0])
        nc.sync.dma_start(offsets[:], offs)
        nc.sync.dma_start(x_planes[1][:], x_rows[1])
        for q in range(4):
            nc.sync.dma_start(
                scales_raw[32 * q + WG_ROW : 32 * q + WG_ROW + 4, :].bitcast(I32),
                wg_scales[0, 4 * q : 4 * q + 4, :].bitcast(I32),
            )
        nc.sync.dma_start(x_planes[2][:], x_rows[2])
        nc.sync.dma_start(x_planes[3][:], x_rows[3])
        for q in range(4):
            nc.sync.dma_start(
                scales_raw[32 * q : 32 * q + 4, :].bitcast(I32).rearrange("r (a n) -> r a n", a=HALVES),
                wd_scales[:, 4 * q : 4 * q + 4, :].bitcast(I32).rearrange("a r n -> r a n"),
            )
        load_wu(0)
        load_wu(1)
        for a in range(HALVES):
            nc.sync.dma_start(wg_raw[a][:], wg_rows[:, a * PASS : (a + 1) * PASS])
        load_wu(2)
        load_wu(3)
        nc.sync.dma_start(wd_raw[:].bitcast(I32).rearrange("p (a w) -> p a w", a=HALVES), wd_words.bitcast(I32).rearrange("a p w -> p a w"))
        load_res(0)

        picked = tile([P, PACK, J], F32, "picked")
        x_codes = tile([P, J], U32, "x_codes")
        x_scales = tile([P, J], U8, "x_scales")
        wu_codes = [tile([P, PASS], U32, f"wu_codes{a}") for a in range(HALVES)]
        wu_scales = [tile([P, PASS], U8, f"wu_scales{a}") for a in range(HALVES)]
        wg_codes = [tile([P, PASS], I32, f"wg_codes{a}") for a in range(HALVES)]
        wd_codes = tile([P, HALVES * N * 2], U8, "wd_codes")
        w_scales = {}
        h_rounded = [tile([P, HALVES * SLICE * PACK], BF16, f"h_rounded{s}") for s in range(SLICES)]
        h_codes = {}
        h_scales = [tile([P, HALVES * SLICE], U8, f"h_scales{s}") for s in range(SLICES)]
        out_codes = tile([P, J], U32, "out_codes")
        out_scales = tile([P, J], U8, "out_scales")

        def h_place(a, c):
            s, half = divmod(c, 2)
            return s, a * SLICE + half * CHUNK

        def gather(i, j0, width):
            entries = offsets[:, j0 // GROUP : (j0 + width) // GROUP]
            nc.vector.tensor_tensor(picked[:, i, j0 : j0 + width], x_planes[i][:].indirect(entries), weights[:, j0 : j0 + width], MULT)

        def interleave(rounded, planes, copy=nc.scalar.copy):
            copy(
                rounded.rearrange("p (c e t) -> p c t e", e=4, t=PACK),
                planes.rearrange("p t (c e) -> p c t e", e=4),
            )

        def quantise_x(j0, width):
            rounded = tile([P, width * PACK], BF16, X_ROUNDED_IN[j0])
            cols = slice(j0, j0 + width)
            interleave(rounded[:], picked[:, :, cols], nc.vector.tensor_copy if j0 == SLICE else nc.scalar.copy)
            nc.vector.quantize_mx(x_codes[:, cols].bitcast(FP8X4), x_scales[:, cols], rounded[:])

        def quantise_wu(a):
            rounded = tile([P, PASS * PACK], BF16, f"wu_rounded{a}")
            places = WU_PIECE // PACK
            for u in range(PASS // WU_PIECE):
                nc.scalar.activation(
                    rounded[:].rearrange("p (t m i) -> p m i t", t=PACK, i=PACK)[:, u * places : (u + 1) * places],
                    wu_raw[2 * a + u][:].rearrange("p i (m t) -> p m i t", t=PACK),
                    COPY,
                )
            nc.vector.quantize_mx(wu_codes[a][:].bitcast(FP8X4), wu_scales[a][:], rounded[:])

        def deal_wg(a):
            nc.vector.tensor_copy(
                wg_codes[a][:].rearrange("p (t c e) -> p c t e", t=PACK, e=4),
                wg_raw[a][:].rearrange("p (c e t) -> p c t e", t=PACK, e=4),
            )

        def deal_scales(a):
            w_scales[a] = tile([P, PASS], U8, W_SCALES_IN[a])
            nc.vector.tensor_copy(
                w_scales[a][:].rearrange("p (t m) -> p t m", t=PACK),
                scales_raw[:, a * PASS : (a + 1) * PASS].rearrange("p (m t) -> p t m", t=PACK),
            )

        def deal_wd():
            nc.vector.tensor_copy(
                wd_codes[:].bitcast(U16).rearrange("p (a t m) -> p a t m", a=HALVES, t=PACK),
                wd_raw[:].bitcast(U16).rearrange("p (a m t) -> p a t m", a=HALVES, t=PACK),
            )

        def sums_with_x(bank, codes, scales, c):
            cols = slice(c * CHUNK, (c + 1) * CHUNK)
            for t in range(PACK):
                nc.tensor.matmul_mx(
                    bank[:, t, :],
                    lhsT=codes[:, t * P : (t + 1) * P].bitcast(FP8X4),
                    lhsT_scale=scales[:, t * P : (t + 1) * P],
                    rhs=x_codes[:, cols].bitcast(FP8X4),
                    rhs_scale=x_scales[:, cols],
                    start=True,
                    stop=True,
                )

        def hidden(a, c):
            def up_sums():
                if (a, c) == (HALVES - 1, CHUNKS - 1):
                    bank = psum.tile([P, PACK, CHUNK], F32, name="y", tag="y", bufs=Y_BANKS)
                else:
                    bank = psum.tile([P, PACK, CHUNK], F32, name="up", tag="up", bufs=UP_BANKS)
                sums_with_x(bank, wu_codes[a][:], wu_scales[a][:], c)
                return bank

            up = up_sums() if c * CHUNK >= SLICE else None
            opened = ring.tile([P, CHUNK // 2, PACK, 2], F32, name="opened", align_bytes=ALIGN)
            gate = psum.tile([P, PACK, CHUNK], F32, name="gate", tag="gate", bufs=GATE_BANKS)
            sums_with_x(gate, wg_codes[a][:], w_scales[a][WG_ROW:P, :], c)
            nc.scalar.activation(opened[:], gate[:].rearrange("p t (c e) -> p c t e", e=2), RELU)
            if up is None:
                up = up_sums()
            s, at = h_place(a, c)
            nc.vector.tensor_tensor(
                h_rounded[s][:, at * PACK : (at + CHUNK) * PACK].rearrange("p (c e t) -> p c t e", e=2, t=PACK),
                up[:].rearrange("p t (c e) -> p c t e", e=2),
                opened[:],
                MULT,
            )

        def quantise_h(s, at, width):
            cols = slice(at, at + width)
            if s not in h_codes:
                h_codes[s] = tile([P, HALVES * SLICE], U32, H_CODES_IN[s])
            nc.vector.quantize_mx(h_codes[s][:, cols].bitcast(FP8X4), h_scales[s][:, cols], h_rounded[s][:, at * PACK : (at + width) * PACK])

        starts = [sum(OUT_WIDTHS[:u]) for u in range(len(OUT_WIDTHS))]
        last = SLICES - 1
        results = {u: tile([P, PACK, OUT_WIDTHS[u]], F32, f"result{u}") for u in (last - 1, last + 1)}

        def down(c):
            if c >= CHUNKS - 2:
                y = psum.tile([P, PACK, CHUNK], F32, name="gate", tag="gate", bufs=GATE_BANKS)
            else:
                y = psum.tile([P, PACK, CHUNK], F32, name="y", tag="y", bufs=Y_BANKS)
            for a in range(HALVES):
                s, at = h_place(a, c)
                cols = slice(at, at + CHUNK)
                for t in range(PACK):
                    nc.tensor.matmul_mx(
                        y[:, t, :],
                        lhsT=wd_codes[:, 2 * (a * PASS + t * P) : 2 * (a * PASS + (t + 1) * P)].bitcast(FP4X4),
                        lhsT_scale=w_scales[a][:, t * P : (t + 1) * P],
                        rhs=h_codes[s][:, cols].bitcast(FP8X4),
                        rhs_scale=h_scales[s][:, cols],
                        start=(a == 0 and t == 0),
                        stop=(a == HALVES - 1 and t == PACK - 1),
                    )
            return y

        staged = {}
        chunk_results = {}
        out_rounded = [tile([P, w * PACK], BF16, f"out_rounded{u}") for u, w in enumerate(OUT_WIDTHS)]

        def res_of(c):
            s, half = divmod(c, 2)
            return res_tiles[s][:, :, half * CHUNK : (half + 1) * CHUNK]

        def store_chunk(c, result):
            nc.sync.dma_start(out_rows[:, :, c * CHUNK : (c + 1) * CHUNK], result[:])
            chunk_results[c] = result

        def round_chunk(c):
            s, half = divmod(c, 2)
            interleave(out_rounded[s][:, half * CHUNK * PACK : (half + 1) * CHUNK * PACK], chunk_results[c][:])

        def add_staged(c):
            result = tile([P, PACK, CHUNK], F32, f"h_rounded{c // 2 + 1}")
            nc.gpsimd.tensor_tensor(result[:], staged[c][:], res_of(c), ADD)
            store_chunk(c, result)

        def add_res(c, y):
            u = max(v for v in range(len(starts)) if starts[v] <= c * CHUNK)
            at = c * CHUNK - starts[u]
            if c in GPSIMD_CHUNKS:
                staged[c] = tile([P, PACK, CHUNK], F32, f"y_staged{c}")
                nc.scalar.copy(staged[c][:], y[:])
            elif u < CHUNKWISE_SLICES:
                result = tile([P, PACK, CHUNK], F32, f"result_odd{c}")
                nc.vector.tensor_tensor(result[:], y[:], res_of(c), ADD)
                store_chunk(c, result)
            else:
                nc.vector.tensor_tensor(results[u][:, :, at : at + CHUNK], y[:], res_of(c), ADD)
                if at + CHUNK == OUT_WIDTHS[u]:
                    nc.sync.dma_start(out_rows[:, :, starts[u] : starts[u] + OUT_WIDTHS[u]], results[u][:])
                    interleave(out_rounded[u][:], results[u][:], nc.vector.tensor_copy if c == CHUNKS - 1 else nc.scalar.copy)

        def quantise_out(u):
            cols = slice(starts[u], starts[u] + OUT_WIDTHS[u])
            if u == 0:
                first_codes = tile([P, SLICE], U32, "res1")
                nc.vector.quantize_mx(first_codes[:].bitcast(FP8X4), out_scales[:, cols], out_rounded[u][:])
                nc.sync.dma_start(out_words[:, cols], first_codes[:].bitcast(I32))
                return
            nc.vector.quantize_mx(out_codes[:, cols].bitcast(FP8X4), out_scales[:, cols], out_rounded[u][:])
            if cols.stop % SLICE == 0:
                whole = slice(cols.stop - SLICE, cols.stop)
                nc.sync.dma_start(out_words[:, whole], out_codes[:, whole].bitcast(I32))

        turned = psum.tile([P, P], F32, name="turned", tag="y", bufs=Y_BANKS)
        nc.tensor.transpose(turned[:], head_rows[:], identity[:])
        u0 = 0
        for part, count in enumerate(SPREAD_PARTS):
            spread = tile([P, count, HEADS, GROUP], F32, f"spread{part}")
            nc.scalar.copy(spread[:], turned[:, 0:live].rearrange("e (g u) -> e u g", u=CHUNKS)[:, u0 : u0 + count, :].unsqueeze(3).to_broadcast([P, count, HEADS, GROUP]))
            back = psum.tile([P, count, P], F32, name="back", tag="gate", bufs=GATE_BANKS)
            for u in range(count):
                nc.tensor.transpose(back[:, u, :], spread[:, u].rearrange("e g v -> e (g v)"), identity[:])
            (nc.vector.tensor_copy if part == 0 else nc.scalar.copy)(weights[:, u0 * P : (u0 + count) * P], back[:].rearrange("p u e -> p (u e)"))
            gather(0, u0 * P, count * P)
            u0 = u0 + count
        for i in range(1, PACK - 1):
            gather(i, 0, J)
        gather(PACK - 1, 0, CHUNK)
        gather(PACK - 1, CHUNK, J - CHUNK)
        quantise_x(0, CHUNK)
        deal_scales(0)
        for s in range(1, SLICES):
            load_res(s)
        deal_wg(0)
        quantise_wu(0)
        deal_wg(1)
        quantise_x(CHUNK, CHUNK)

        hidden(0, 0)
        deal_scales(1)
        hidden(0, 1)
        quantise_x(SLICE, SLICE)
        deal_wd()
        quantise_wu(1)
        hidden(1, 0)
        hidden(1, 1)
        for s in range(1, SLICES):
            c = 2 * s
            if s < last:
                quantise_x((s + 1) * SLICE, SLICE)
            hidden(0, c)
            quantise_h(s - 1, 0, HALVES * SLICE)
            if s > 1:
                add_staged(c - 4)
            sums = [down(c - 2), down(c - 1)]
            hidden(0, c + 1)
            add_res(c - 2, sums[0])
            hidden(1, c)
            add_res(c - 1, sums[1])
            if s > 1:
                round_chunk(c - 3)
                round_chunk(c - 4)
            if s == last:
                quantise_h(s, 0, SLICE + CHUNK)
            hidden(1, c + 1)
        sums = [down(CHUNKS - 2)]
        quantise_out(0)
        quantise_h(last, SLICE + CHUNK, CHUNK)
        sums.append(down(CHUNKS - 1))
        results[last] = tile([P, PACK, CHUNK], F32, f"h_rounded{last}")
        add_res(CHUNKS - 2, sums[0])
        quantise_out(last - 2)
        add_res(CHUNKS - 1, sums[1])
        quantise_out(last - 1)
        quantise_out(last)
        quantise_out(last + 1)

        queues = (nc.sync, nc.scalar, nc.sync, nc.scalar)
        for q in range(4):
            queues[q].dma_start(
                out_2[0, 4 * q : 4 * q + 4, :].bitcast(I32), out_scales[32 * q : 32 * q + 4, :].bitcast(I32)
            )
